import numpy as np
import ml_dtypes


def mxq(x, axis, fmt="e4m3"):
    dtype, down = {"e4m3": (ml_dtypes.float8_e4m3fn, 7), "e5m2": (ml_dtypes.float8_e5m2, 14)}[fmt]
    v = np.moveaxis(np.asarray(x, np.float32).astype(ml_dtypes.bfloat16).astype(np.float64), axis, -1)
    blocks = v.reshape(v.shape[:-1] + (-1, 32))
    amax = np.abs(blocks).max(-1, keepdims=True)
    byte = np.maximum(np.where(amax > 0, np.frexp(amax)[1] - 1 + 127, 0) - down, 1)
    scale = np.exp2(byte - 127.0)
    codes = (blocks / scale).astype(np.float32).astype(dtype).astype(np.float64)
    return np.moveaxis((codes * scale).reshape(v.shape), -1, axis)


WIDE = False


def mx_kscale(k):
    if not WIDE:
        return np.ones(k)
    levels = np.array([10, -10, 5, -5, 0])
    if k % 512:
        return np.exp2(np.random.permutation(np.resize(levels, k // 32))).repeat(32)
    a = np.empty((k // 512, 16))
    for p in range(k // 512):
        a[p, :8] = np.random.permutation(np.resize(levels, 8))
        for g in range(8):
            far = levels[np.abs(levels - a[p, g]) >= 10]
            a[p, g + 8] = far[np.random.randint(len(far))]
    return np.exp2(a.ravel()).repeat(32)


def f64(x):
    return np.asarray(x).astype(np.float64)


def striped(idx):
    return np.tile(idx.reshape(-1, 16).T, (8, 1)).astype(np.uint16)


def unstriped(offs):
    return offs[:16].T.reshape(-1).astype(np.int64)


def pack_weight(w):
    k, n = w.shape
    w = f64(np.asarray(w, np.float32).astype(ml_dtypes.bfloat16)).reshape(k // 32, 32, n)
    amax = np.abs(w).max(1)
    byte = np.clip(np.where(amax > 0, np.frexp(amax)[1] - 1 + 127 - 7, 1), 1, 254)
    scaled = (w * np.exp2(127.0 - byte)[:, None, :]).reshape(k, n).astype(np.float32)
    words = np.ascontiguousarray(scaled.reshape(k // 512, 128, 4, n).transpose(0, 1, 3, 2)).astype(ml_dtypes.float8_e4m3fn).view(np.uint8)
    return words, np.ascontiguousarray(byte.astype(np.uint8).reshape(k // 512, 16, n))


def unpack_weight(words, scales):
    g, p, n, _ = words.shape
    vals = np.ascontiguousarray(words).view(ml_dtypes.float8_e4m3fn).astype(np.float64) * np.repeat(np.exp2(scales.astype(np.float64) - 127.0), 8, axis=1)[..., None]
    return vals.transpose(0, 1, 3, 2).reshape(g * 512, n)


K, T, S, V, U, R = 512, 4096, 1024, 512, 512, 256
P = 2 ** 7


def setup_inputs():
    n = np.random.standard_normal
    s = mx_kscale(K)[:, None]
    packed_xT = pack_weight(n((K, T)) * s)
    return {
        "x_words": packed_xT[0],
        "x_scales": packed_xT[1],
        "hT": (n((K, V)) / np.sqrt(K) / s).astype(np.float32),
        "norm": (np.tile(np.random.uniform(0.5, 2.0, U), (P, 1))).astype(np.float32),
        "offs": striped(np.random.permutation(T)[:S]),
        "code1": striped(np.random.permutation(np.concatenate([np.arange(R), np.random.randint(0, R, U - R)]))),
        "code2": striped(np.random.permutation(np.concatenate([np.arange(R), np.random.randint(0, R, U - R)]))),
        "code3": striped(np.random.permutation(np.concatenate([np.arange(R), np.random.randint(0, R, U - R)]))),
        "code4": striped(np.random.permutation(np.concatenate([np.arange(R), np.random.randint(0, R, U - R)]))),
    }


def reference(x_words, x_scales, hT, norm, offs, code1, code2, code3, code4):
    hTq = mxq(f64(hT), 0, "e4m3")
    xq = unpack_weight(x_words, x_scales)[:, unstriped(offs)]
    y = hTq.T @ xq
    l0 = y[:, :R]
    l1 = y[:, R:2 * R]
    l2 = y[:, 2 * R:3 * R]
    l3 = y[:, 3 * R:4 * R]
    return l0[:, unstriped(code1)] + l1[:, unstriped(code2)] + l2[:, unstriped(code3)] + l3[:, unstriped(code4)] - f64(norm)[:1]

@@ -1,0 +1,188 @@
+from contextlib import ExitStack
+
+import concourse.mybir as mybir
+
+K, T, S, V, U, R = 512, 4096, 1024, 512, 512, 256
+BOOKS = 4
+FLOPS = 2 * K * V * S
+
+F32 = mybir.dt.float32
+BF16 = mybir.dt.bfloat16
+I32 = mybir.dt.int32
+U32 = mybir.dt.uint32
+U16 = mybir.dt.uint16
+U8 = mybir.dt.uint8
+FP8X4 = mybir.dt.float8_e4m3fn_x4
+ADD = mybir.AluOpType.add
+SUBTRACT = mybir.AluOpType.subtract
+
+P = 128
+PACK = 4
+LIST_ROWS = 16
+HALF = S // 2
+BLOCKS = V // P
+FIRST_WINDOW = 2 * U
+LATER_WINDOW = U + 16
+
+
+def tile_picked_yadc_dist_p_kernel(
+    tc, x_words, x_scales, hT, norm, offs, code1, code2, code3, code4, out
+):
+    nc = tc.nc
+    with ExitStack() as ctx:
+        keep = ctx.enter_context(tc.tile_pool(name="keep", bufs=1))
+        psum = ctx.enter_context(tc.psum_pool(name="psum", bufs=1))
+
+        picks = keep.tile([P, S // LIST_ROWS], U16, name="picks")
+        nc.sync.dma_start(picks[:], offs)
+
+        store_words = keep.tile([P, T], U32, name="store_words")
+        nc.sync.dma_start(
+            store_words[:].bitcast(I32), x_words[0].rearrange("p n t -> p (n t)").bitcast(I32)
+        )
+
+        store_scales = keep.tile([P, T], U8, name="store_scales", tag="shared0", align_bytes=64)
+        nc.vector.memset(store_scales[:].bitcast(I32), 0)
+        for q in range(4):
+            nc.scalar.dma_start(
+                store_scales[32 * q : 32 * q + 4, :].bitcast(I32),
+                x_scales[0, 4 * q : 4 * q + 4, :].bitcast(I32),
+            )
+
+        h_rows = hT.rearrange("(p j) t -> p j t", j=PACK)
+        groups = [(0, 1), (1, 2), (2, 4)]
+        raws = [
+            keep.tile([P, PACK, (hi - lo) * P], F32, name="raw%d" % lo) for lo, hi in groups
+        ]
+        codes = [keep.tile([P, U // LIST_ROWS], U16, name="code%d" % d) for d in range(BOOKS)]
+        norm_rows = keep.tile([P, U], F32, name="norm_rows")
+
+        def load_queries(g):
+            lo, hi = groups[g]
+            nc.sync.dma_start(raws[g][:], h_rows[:, :, lo * P : hi * P])
+
+        load_queries(0)
+        nc.sync.dma_start(codes[0][:], code1)
+        load_queries(1)
+        nc.sync.dma_start(norm_rows[:], norm)
+        nc.sync.dma_start(codes[1][:], code2)
+        nc.sync.dma_start(codes[2][:], code3)
+        nc.sync.dma_start(codes[3][:], code4)
+        load_queries(2)
+
+        windows = [
+            [
+                keep.tile(
+                    [P, FIRST_WINDOW if d == 0 else LATER_WINDOW], F32, name="table%d_%d" % (s, d)
+                )
+                for d in range(BOOKS)
+            ]
+            for s in range(2)
+        ]
+        for s in range(2):
+            nc.vector.memset(windows[s][0][:, R:], 0.0)
+        for s in range(2):
+            for d in range(1, BOOKS):
+                nc.scalar.copy(windows[s][d][:, R:], windows[0][0][:, R : R + LATER_WINDOW - R])
+
+        picked_scales = keep.tile([P, S], U8, name="picked_scales", align_bytes=64)
+        nc.vector.tensor_copy(picked_scales[:], store_scales[:].indirect(picks[:]))
+        picked_words = {}
+        h_codes = keep.tile([P, V], U32, name="h_codes", align_bytes=64)
+        h_scales = keep.tile([P, V], U8, name="h_scales", align_bytes=64)
+        grouped = [
+            keep.tile(
+                [P, (hi - lo) * P, PACK],
+                BF16,
+                name="grouped%d" % lo,
+                tag="shared1" if lo == 0 else "grouped%d" % lo,
+                align_bytes=64,
+            )
+            for lo, hi in groups
+        ]
+
+        def pick_words(h):
+            cols = HALF // LIST_ROWS
+            picked_words[h] = keep.tile(
+                [P, HALF], U32, name="picked_words%d" % h, tag="shared%d" % h, align_bytes=64
+            )
+            nc.vector.tensor_copy(
+                picked_words[h][:], store_words[:].indirect(picks[:, h * cols : (h + 1) * cols])
+            )
+
+        def interleave(g):
+            nc.scalar.copy(
+                grouped[g][:].rearrange("p (c i) j -> p c j i", i=4),
+                raws[g][:].rearrange("p j (c i) -> p c j i", i=4),
+            )
+
+        def quantise(g):
+            lo, hi = groups[g]
+            nc.vector.quantize_mx(
+                out=h_codes[:, lo * P : hi * P].bitcast(FP8X4),
+                scales=h_scales[:, lo * P : hi * P],
+                in_=grouped[g][:].rearrange("p t j -> p (t j)"),
+            )
+
+        banks = {}
+
+        def multiply(b, h):
+            banks[b, h] = psum.tile([P, HALF], F32, name="bank%d_%d" % (b, h))
+            nc.tensor.matmul_mx(
+                out=banks[b, h][:],
+                lhsT=h_codes[:, b * P : (b + 1) * P].bitcast(FP8X4),
+                lhsT_scale=h_scales[:, b * P : (b + 1) * P],
+                rhs=picked_words[h][:].bitcast(FP8X4),
+                rhs_scale=picked_scales[:, h * HALF : (h + 1) * HALF],
+                start=True,
+                stop=True,
+            )
+
+        def fill_table(b, d):
+            nc.scalar.copy(
+                windows[b % 2][d][:, :R], banks[b, d // 2][:, (d % 2) * R : (d % 2 + 1) * R]
+            )
+
+        sums = {}
+
+        def look_up(b, d):
+            sums[b, d] = keep.tile([P, U], F32, name="sum%d_%d" % (b, d))
+            entries = windows[b % 2][d][:].indirect(codes[d][:])
+            if d == 0:
+                nc.vector.tensor_tensor(sums[b, d][:], entries, norm_rows[:], SUBTRACT)
+            else:
+                nc.vector.tensor_tensor(sums[b, d][:], entries, sums[b, d - 1][:], ADD)
+            if d == BOOKS - 1:
+                nc.sync.dma_start(out[b * P : (b + 1) * P, :], sums[b, d][:])
+
+        pick_words(0)
+        interleave(0)
+        quantise(0)
+        multiply(0, 0)
+        fill_table(0, 0)
+        pick_words(1)
+        interleave(1)
+        quantise(1)
+        multiply(1, 0)
+        multiply(0, 1)
+        multiply(1, 1)
+        fill_table(1, 0)
+        for d in range(1, BOOKS):
+            fill_table(0, d)
+            fill_table(1, d)
+        interleave(2)
+        look_up(0, 0)
+        look_up(1, 0)
+        quantise(2)
+        for h in range(2):
+            multiply(2, h)
+            multiply(3, h)
+        fill_table(2, 0)
+        fill_table(3, 0)
+        for d in range(1, BOOKS):
+            for b in (0, 1):
+                look_up(b, d)
+                fill_table(b + 2, d)
+        for d in range(BOOKS):
+            for b in (2, 3):
+                look_up(b, d)

@@ -36,39 +36,22 @@ def tile_picked_yadc_dist_p_kernel(
         picks = keep.tile([P, S // LIST_ROWS], U16, name="picks")
         nc.sync.dma_start(picks[:], offs)
 
-        store_words = keep.tile([P, T], U32, name="store_words")
-        nc.sync.dma_start(
-            store_words[:].bitcast(I32), x_words[0].rearrange("p n t -> p (n t)").bitcast(I32)
-        )
-
-        store_scales = keep.tile([P, T], U8, name="store_scales", tag="shared0", align_bytes=64)
-        nc.vector.memset(store_scales[:].bitcast(I32), 0)
-        for q in range(4):
-            nc.scalar.dma_start(
-                store_scales[32 * q : 32 * q + 4, :].bitcast(I32),
-                x_scales[0, 4 * q : 4 * q + 4, :].bitcast(I32),
-            )
+        codes = [keep.tile([P, U // LIST_ROWS], U16, name="code%d" % d) for d in range(BOOKS)]
 
         h_rows = hT.rearrange("(p j) t -> p j t", j=PACK)
-        groups = [(0, 1), (1, 2), (2, 4)]
-        raws = [
-            keep.tile([P, PACK, (hi - lo) * P], F32, name="raw%d" % lo) for lo, hi in groups
-        ]
-        codes = [keep.tile([P, U // LIST_ROWS], U16, name="code%d" % d) for d in range(BOOKS)]
-        norm_rows = keep.tile([P, U], F32, name="norm_rows")
+        loads = [(0, 1), (1, 2), (2, 4)]
+        raws = {}
 
         def load_queries(g):
-            lo, hi = groups[g]
-            nc.sync.dma_start(raws[g][:], h_rows[:, :, lo * P : hi * P])
+            lo, hi = loads[g]
+            raw = keep.tile([P, PACK, (hi - lo) * P], F32, name="raw%d" % g, tag="spread" if g == 2 else "raw")
+            nc.sync.dma_start(raw[:], h_rows[:, :, lo * P : hi * P])
+            for b in range(lo, hi):
+                raws[b] = raw[:, :, (b - lo) * P : (b - lo + 1) * P]
 
         load_queries(0)
-        nc.sync.dma_start(codes[0][:], code1)
-        load_queries(1)
-        nc.sync.dma_start(norm_rows[:], norm)
-        nc.sync.dma_start(codes[1][:], code2)
-        nc.sync.dma_start(codes[2][:], code3)
-        nc.sync.dma_start(codes[3][:], code4)
-        load_queries(2)
+        for tile, code in zip(codes, (code1, code2, code3, code4)):
+            nc.sync.dma_start(tile[:], code)
 
         windows = [
             [
@@ -79,33 +62,49 @@ def tile_picked_yadc_dist_p_kernel(
             ]
             for s in range(2)
         ]
+        zeros = keep.tile([P, LATER_WINDOW - U], F32, name="zeros", tag="words")
+        nc.vector.memset(zeros[:], 0.0)
+        store_scales = keep.tile([P, T], U8, name="store_scales")
+        nc.vector.memset(store_scales[:].bitcast(I32), 0)
+        nc.sync.dma_start(store_scales[0:P:8, :].bitcast(I32), x_scales[0].bitcast(I32))
+        nc.vector.tensor_copy(windows[0][1][:, U:], zeros[:])
+
+        store_words = keep.tile([P, T], U32, name="store_words", tag="words")
+        nc.sync.dma_start(
+            store_words[:].bitcast(I32), x_words[0].rearrange("p n t -> p (n t)").bitcast(I32)
+        )
+
+        picked_scales = keep.tile([P, S], U8, name="picked_scales", align_bytes=64)
+        nc.vector.memset(picked_scales[:].bitcast(I32), 0)
+        nc.vector.memset(windows[0][1][:, R:U], 0.0)
         for s in range(2):
             nc.vector.memset(windows[s][0][:, R:], 0.0)
         for s in range(2):
             for d in range(1, BOOKS):
-                nc.scalar.copy(windows[s][d][:, R:], windows[0][0][:, R : R + LATER_WINDOW - R])
+                if (s, d) != (0, 1):
+                    nc.scalar.copy(windows[s][d][:, R:], windows[0][1][:, R:])
 
-        picked_scales = keep.tile([P, S], U8, name="picked_scales", align_bytes=64)
-        nc.vector.tensor_copy(picked_scales[:], store_scales[:].indirect(picks[:]))
-        picked_words = {}
+        spread_scales = keep.tile([P, S], U8, name="spread_scales", tag="spread")
+        nc.vector.tensor_copy(spread_scales[:], store_scales[:].indirect(picks[:]))
+        for r in range(4):
+            nc.scalar.dma_start(
+                picked_scales[r:P:32, :].bitcast(I32),
+                spread_scales[8 * r : P : 32, :].bitcast(I32),
+            )
+        load_queries(2)
+
+        picked_words = [
+            keep.tile([P, HALF], U32, name="picked_words%d" % h, align_bytes=64) for h in range(2)
+        ]
         h_codes = keep.tile([P, V], U32, name="h_codes", align_bytes=64)
         h_scales = keep.tile([P, V], U8, name="h_scales", align_bytes=64)
         grouped = [
-            keep.tile(
-                [P, (hi - lo) * P, PACK],
-                BF16,
-                name="grouped%d" % lo,
-                tag="shared1" if lo == 0 else "grouped%d" % lo,
-                align_bytes=64,
-            )
-            for lo, hi in groups
+            keep.tile([P, P, PACK], BF16, name="grouped%d" % b, tag="g%d" % b, align_bytes=64)
+            for b in range(BLOCKS)
         ]
 
         def pick_words(h):
             cols = HALF // LIST_ROWS
-            picked_words[h] = keep.tile(
-                [P, HALF], U32, name="picked_words%d" % h, tag="shared%d" % h, align_bytes=64
-            )
             nc.vector.tensor_copy(
                 picked_words[h][:], store_words[:].indirect(picks[:, h * cols : (h + 1) * cols])
             )
@@ -113,11 +112,11 @@ def tile_picked_yadc_dist_p_kernel(
         def interleave(g):
             nc.scalar.copy(
                 grouped[g][:].rearrange("p (c i) j -> p c j i", i=4),
-                raws[g][:].rearrange("p j (c i) -> p c j i", i=4),
+                raws[g].rearrange("p j (c i) -> p c j i", i=4),
             )
 
         def quantise(g):
-            lo, hi = groups[g]
+            lo, hi = g, g + 1
             nc.vector.quantize_mx(
                 out=h_codes[:, lo * P : hi * P].bitcast(FP8X4),
                 scales=h_scales[:, lo * P : hi * P],
@@ -146,18 +145,27 @@ def tile_picked_yadc_dist_p_kernel(
         sums = {}
 
         def look_up(b, d):
-            sums[b, d] = keep.tile([P, U], F32, name="sum%d_%d" % (b, d))
-            entries = windows[b % 2][d][:].indirect(codes[d][:])
-            if d == 0:
-                nc.vector.tensor_tensor(sums[b, d][:], entries, norm_rows[:], SUBTRACT)
-            else:
-                nc.vector.tensor_tensor(sums[b, d][:], entries, sums[b, d - 1][:], ADD)
-            if d == BOOKS - 1:
-                nc.sync.dma_start(out[b * P : (b + 1) * P, :], sums[b, d][:])
+            tag = "g%d" % (b + 2) if b < 2 and d == 3 else "sum%d_%d" % (b, d)
+            sums[b, d] = keep.tile([P, U], F32, name="sum%d_%d" % (b, d), tag=tag, align_bytes=64)
+            pieces = 2 if (b, d) == (BLOCKS - 1, BOOKS - 1) else 1
+            width = U // pieces
+            for i in range(pieces):
+                cols = slice(i * width, (i + 1) * width)
+                offsets = codes[d][:, i * width // LIST_ROWS : (i + 1) * width // LIST_ROWS]
+                entries = windows[b % 2][d][:].indirect(offsets)
+                if d == 0:
+                    nc.vector.tensor_tensor(sums[b, d][:, cols], entries, norm_rows[:, cols], SUBTRACT)
+                else:
+                    nc.vector.tensor_tensor(sums[b, d][:, cols], entries, sums[b, d - 1][:, cols], ADD)
+                if d == BOOKS - 1:
+                    nc.sync.dma_start(out[b * P : (b + 1) * P, cols], sums[b, d][:, cols])
 
-        pick_words(0)
         interleave(0)
+        load_queries(1)
         quantise(0)
+        norm_rows = keep.tile([P, U], F32, name="norm_rows", tag="g0", align_bytes=64)
+        nc.sync.dma_start(norm_rows[:], norm)
+        pick_words(0)
         multiply(0, 0)
         fill_table(0, 0)
         pick_words(1)
@@ -171,9 +179,11 @@ def tile_picked_yadc_dist_p_kernel(
             fill_table(0, d)
             fill_table(1, d)
         interleave(2)
+        interleave(3)
         look_up(0, 0)
         look_up(1, 0)
         quantise(2)
+        quantise(3)
         for h in range(2):
             multiply(2, h)
             multiply(3, h)

@@ -23,6 +23,7 @@ HALF = S // 2
 BLOCKS = V // P
 FIRST_WINDOW = 2 * U
 LATER_WINDOW = U + 16
+BLOCK_BYTES = PACK * P * 4
 
 
 def tile_picked_yadc_dist_p_kernel(
@@ -31,128 +32,110 @@ def tile_picked_yadc_dist_p_kernel(
     nc = tc.nc
     with ExitStack() as ctx:
         keep = ctx.enter_context(tc.tile_pool(name="keep", bufs=1))
+        late = ctx.enter_context(tc.tile_pool(name="late", bufs=1))
+        head = ctx.enter_context(tc.tile_pool(name="head", bufs=1))
         psum = ctx.enter_context(tc.psum_pool(name="psum", bufs=1))
 
+        h_rows = hT.rearrange("(p j) t -> p j t", j=PACK)
+        raw0 = keep.tile([P, PACK, P], F32, name="raw0")
+        nc.scalar.dma_start(raw0[:], h_rows[:, :, :P])
+        store_words = keep.tile([P, T], U32, name="store_words")
+        nc.scalar.dma_start(
+            store_words[:].bitcast(I32), x_words[0].rearrange("p n t -> p (n t)").bitcast(I32)
+        )
         picks = keep.tile([P, S // LIST_ROWS], U16, name="picks")
         nc.sync.dma_start(picks[:], offs)
 
+        store_scales = head.tile([P, T], U8, name="store_scales", offset=0, align_bytes=64)
+        nc.vector.memset(store_scales[:].bitcast(I32), 0)
+        nc.sync.dma_start(store_scales[32:96:4, :].bitcast(I32), x_scales[0].bitcast(I32))
+
         codes = [keep.tile([P, U // LIST_ROWS], U16, name="code%d" % d) for d in range(BOOKS)]
-
-        h_rows = hT.rearrange("(p j) t -> p j t", j=PACK)
-        loads = [(0, 1), (1, 2), (2, 4)]
-        raws = {}
-
-        def load_queries(g):
-            lo, hi = loads[g]
-            raw = keep.tile([P, PACK, (hi - lo) * P], F32, name="raw%d" % g, tag="spread" if g == 2 else "raw")
-            nc.sync.dma_start(raw[:], h_rows[:, :, lo * P : hi * P])
-            for b in range(lo, hi):
-                raws[b] = raw[:, :, (b - lo) * P : (b - lo + 1) * P]
-
-        load_queries(0)
         for tile, code in zip(codes, (code1, code2, code3, code4)):
             nc.sync.dma_start(tile[:], code)
 
         windows = [
-            [
-                keep.tile(
-                    [P, FIRST_WINDOW if d == 0 else LATER_WINDOW], F32, name="table%d_%d" % (s, d)
-                )
-                for d in range(BOOKS)
-            ]
-            for s in range(2)
+            keep.tile([P, FIRST_WINDOW if d == 0 else LATER_WINDOW], F32, name="table%d" % d)
+            for d in range(BOOKS)
         ]
-        zeros = keep.tile([P, LATER_WINDOW - U], F32, name="zeros", tag="words")
-        nc.vector.memset(zeros[:], 0.0)
-        store_scales = keep.tile([P, T], U8, name="store_scales")
-        nc.vector.memset(store_scales[:].bitcast(I32), 0)
-        nc.sync.dma_start(store_scales[0:P:8, :].bitcast(I32), x_scales[0].bitcast(I32))
-        nc.vector.tensor_copy(windows[0][1][:, U:], zeros[:])
-
-        store_words = keep.tile([P, T], U32, name="store_words", tag="words")
-        nc.sync.dma_start(
-            store_words[:].bitcast(I32), x_words[0].rearrange("p n t -> p (n t)").bitcast(I32)
-        )
+        for i in range(2):
+            zeros = late.tile([P, 16], F32, name="zeros%d" % i, offset=(2 * i + 1) * BLOCK_BYTES - 32)
+            nc.vector.memset(zeros[:], 0.0)
+            nc.scalar.copy(windows[1 + i][:, U:], zeros[:])
+        raws = [raw0]
+        for b in range(1, BLOCKS):
+            raw = late.tile([P, PACK, P], F32, name="raw%d" % b, offset=(0, 0, 2, 3)[b] * BLOCK_BYTES)
+            nc.scalar.dma_start(raw[:], h_rows[:, :, b * P : (b + 1) * P])
+            raws.append(raw)
+            if b == 1:
+                norm_rows = late.tile([P, U], F32, name="norm_rows", offset=BLOCK_BYTES)
+                nc.scalar.dma_start(norm_rows[:], norm)
 
         picked_scales = keep.tile([P, S], U8, name="picked_scales", align_bytes=64)
         nc.vector.memset(picked_scales[:].bitcast(I32), 0)
-        nc.vector.memset(windows[0][1][:, R:U], 0.0)
-        for s in range(2):
-            nc.vector.memset(windows[s][0][:, R:], 0.0)
-        for s in range(2):
-            for d in range(1, BOOKS):
-                if (s, d) != (0, 1):
-                    nc.scalar.copy(windows[s][d][:, R:], windows[0][1][:, R:])
+        nc.vector.memset(windows[0][:, R:], 0.0)
+        for d in (1, 2):
+            nc.vector.memset(windows[d][:, R:U], 0.0)
+        nc.vector.memset(windows[3][:, R:], 0.0)
 
-        spread_scales = keep.tile([P, S], U8, name="spread_scales", tag="spread")
+        spread_scales = keep.tile([P, S], U8, name="spread_scales")
         nc.vector.tensor_copy(spread_scales[:], store_scales[:].indirect(picks[:]))
         for r in range(4):
-            nc.scalar.dma_start(
+            nc.sync.dma_start(
                 picked_scales[r:P:32, :].bitcast(I32),
-                spread_scales[8 * r : P : 32, :].bitcast(I32),
+                spread_scales[32 + 4 * r : 96 : 16, :].bitcast(I32),
             )
-        load_queries(2)
 
-        picked_words = [
-            keep.tile([P, HALF], U32, name="picked_words%d" % h, align_bytes=64) for h in range(2)
-        ]
+        picked_words = head.tile([P, S], U32, name="picked_words", offset=0, align_bytes=64)
         h_codes = keep.tile([P, V], U32, name="h_codes", align_bytes=64)
         h_scales = keep.tile([P, V], U8, name="h_scales", align_bytes=64)
-        grouped = [
-            keep.tile([P, P, PACK], BF16, name="grouped%d" % b, tag="g%d" % b, align_bytes=64)
-            for b in range(BLOCKS)
-        ]
 
         def pick_words(h):
             cols = HALF // LIST_ROWS
             nc.vector.tensor_copy(
-                picked_words[h][:], store_words[:].indirect(picks[:, h * cols : (h + 1) * cols])
+                picked_words[:, h * HALF : (h + 1) * HALF], store_words[:].indirect(picks[:, h * cols : (h + 1) * cols])
             )
 
-        def interleave(g):
-            nc.scalar.copy(
-                grouped[g][:].rearrange("p (c i) j -> p c j i", i=4),
-                raws[g].rearrange("p j (c i) -> p c j i", i=4),
+        def prepare(b):
+            copy = nc.vector.tensor_copy if b == 0 else nc.scalar.copy
+            if b < 2:
+                grouped = head.tile(
+                    [P, P, PACK], BF16, name="grouped%d" % b, offset=T - 512 + 512 * b, align_bytes=64
+                )
+            else:
+                grouped = keep.tile(
+                    [P, P, PACK], BF16, name="grouped%d" % b, tag="sum0_%d" % (b - 2), align_bytes=64
+                )
+            copy(
+                grouped[:].rearrange("p (c i) j -> p c j i", i=4),
+                raws[b][:].rearrange("p j (c i) -> p c j i", i=4),
             )
-
-        def quantise(g):
-            lo, hi = g, g + 1
             nc.vector.quantize_mx(
-                out=h_codes[:, lo * P : hi * P].bitcast(FP8X4),
-                scales=h_scales[:, lo * P : hi * P],
-                in_=grouped[g][:].rearrange("p t j -> p (t j)"),
-            )
-
-        banks = {}
-
-        def multiply(b, h):
-            banks[b, h] = psum.tile([P, HALF], F32, name="bank%d_%d" % (b, h))
-            nc.tensor.matmul_mx(
-                out=banks[b, h][:],
-                lhsT=h_codes[:, b * P : (b + 1) * P].bitcast(FP8X4),
-                lhsT_scale=h_scales[:, b * P : (b + 1) * P],
-                rhs=picked_words[h][:].bitcast(FP8X4),
-                rhs_scale=picked_scales[:, h * HALF : (h + 1) * HALF],
-                start=True,
-                stop=True,
-            )
-
-        def fill_table(b, d):
-            nc.scalar.copy(
-                windows[b % 2][d][:, :R], banks[b, d // 2][:, (d % 2) * R : (d % 2 + 1) * R]
+                out=h_codes[:, b * P : (b + 1) * P].bitcast(FP8X4),
+                scales=h_scales[:, b * P : (b + 1) * P],
+                in_=grouped[:].rearrange("p t j -> p (t j)"),
             )
 
         sums = {}
 
-        def look_up(b, d):
-            tag = "g%d" % (b + 2) if b < 2 and d == 3 else "sum%d_%d" % (b, d)
-            sums[b, d] = keep.tile([P, U], F32, name="sum%d_%d" % (b, d), tag=tag, align_bytes=64)
-            pieces = 2 if (b, d) == (BLOCKS - 1, BOOKS - 1) else 1
+        def look_up(b, d, pieces):
+            bank = psum.tile([P, R], F32, name="bank")
+            nc.tensor.matmul_mx(
+                out=bank[:],
+                lhsT=h_codes[:, b * P : (b + 1) * P].bitcast(FP8X4),
+                lhsT_scale=h_scales[:, b * P : (b + 1) * P],
+                rhs=picked_words[:, d * R : (d + 1) * R].bitcast(FP8X4),
+                rhs_scale=picked_scales[:, d * R : (d + 1) * R],
+                start=True,
+                stop=True,
+            )
+            nc.scalar.copy(windows[d][:, :R], bank[:])
+            sums[b, d] = keep.tile([P, U], F32, name="sum%d_%d" % (b, d), tag="sum%d_%d" % (b, d), align_bytes=64)
             width = U // pieces
             for i in range(pieces):
                 cols = slice(i * width, (i + 1) * width)
                 offsets = codes[d][:, i * width // LIST_ROWS : (i + 1) * width // LIST_ROWS]
-                entries = windows[b % 2][d][:].indirect(offsets)
+                entries = windows[d][:].indirect(offsets)
                 if d == 0:
                     nc.vector.tensor_tensor(sums[b, d][:, cols], entries, norm_rows[:, cols], SUBTRACT)
                 else:
@@ -160,39 +143,13 @@ def tile_picked_yadc_dist_p_kernel(
                 if d == BOOKS - 1:
                     nc.sync.dma_start(out[b * P : (b + 1) * P, cols], sums[b, d][:, cols])
 
-        interleave(0)
-        load_queries(1)
-        quantise(0)
-        norm_rows = keep.tile([P, U], F32, name="norm_rows", tag="g0", align_bytes=64)
-        nc.sync.dma_start(norm_rows[:], norm)
+        prepare(0)
         pick_words(0)
-        multiply(0, 0)
-        fill_table(0, 0)
         pick_words(1)
-        interleave(1)
-        quantise(1)
-        multiply(1, 0)
-        multiply(0, 1)
-        multiply(1, 1)
-        fill_table(1, 0)
-        for d in range(1, BOOKS):
-            fill_table(0, d)
-            fill_table(1, d)
-        interleave(2)
-        interleave(3)
-        look_up(0, 0)
-        look_up(1, 0)
-        quantise(2)
-        quantise(3)
-        for h in range(2):
-            multiply(2, h)
-            multiply(3, h)
-        fill_table(2, 0)
-        fill_table(3, 0)
-        for d in range(1, BOOKS):
-            for b in (0, 1):
-                look_up(b, d)
-                fill_table(b + 2, d)
-        for d in range(BOOKS):
-            for b in (2, 3):
-                look_up(b, d)
+        prepare(1)
+        order = [(0, 0), (0, 1), (1, 0), (0, 2), (1, 1), (0, 3), (1, 2), (2, 0),
+                 (1, 3), (2, 1), (3, 0), (2, 2), (3, 1), (2, 3), (3, 2), (3, 3)]
+        for i, (b, d) in enumerate(order):
+            look_up(b, d, 2 if i < 2 or i >= len(order) - 2 else 1)
+            if b == 0 and d in (1, 2):
+                prepare(d + 1)

@@ -33,23 +33,13 @@ def tile_picked_yadc_dist_p_kernel(
     with ExitStack() as ctx:
         keep = ctx.enter_context(tc.tile_pool(name="keep", bufs=1))
         late = ctx.enter_context(tc.tile_pool(name="late", bufs=1))
-        head = ctx.enter_context(tc.tile_pool(name="head", bufs=1))
         psum = ctx.enter_context(tc.psum_pool(name="psum", bufs=1))
 
+        picks = keep.tile([P, S // LIST_ROWS], U16, name="picks")
+        nc.sync.dma_start(picks[:], offs)
         h_rows = hT.rearrange("(p j) t -> p j t", j=PACK)
         raw0 = keep.tile([P, PACK, P], F32, name="raw0")
         nc.scalar.dma_start(raw0[:], h_rows[:, :, :P])
-        store_words = keep.tile([P, T], U32, name="store_words")
-        nc.scalar.dma_start(
-            store_words[:].bitcast(I32), x_words[0].rearrange("p n t -> p (n t)").bitcast(I32)
-        )
-        picks = keep.tile([P, S // LIST_ROWS], U16, name="picks")
-        nc.sync.dma_start(picks[:], offs)
-
-        store_scales = head.tile([P, T], U8, name="store_scales", offset=0, align_bytes=64)
-        nc.vector.memset(store_scales[:].bitcast(I32), 0)
-        nc.sync.dma_start(store_scales[32:96:4, :].bitcast(I32), x_scales[0].bitcast(I32))
-
         codes = [keep.tile([P, U // LIST_ROWS], U16, name="code%d" % d) for d in range(BOOKS)]
         for tile, code in zip(codes, (code1, code2, code3, code4)):
             nc.sync.dma_start(tile[:], code)
@@ -58,25 +48,23 @@ def tile_picked_yadc_dist_p_kernel(
             keep.tile([P, FIRST_WINDOW if d == 0 else LATER_WINDOW], F32, name="table%d" % d)
             for d in range(BOOKS)
         ]
-        for i in range(2):
-            zeros = late.tile([P, 16], F32, name="zeros%d" % i, offset=(2 * i + 1) * BLOCK_BYTES - 32)
-            nc.vector.memset(zeros[:], 0.0)
-            nc.scalar.copy(windows[1 + i][:, U:], zeros[:])
-        raws = [raw0]
-        for b in range(1, BLOCKS):
-            raw = late.tile([P, PACK, P], F32, name="raw%d" % b, offset=(0, 0, 2, 3)[b] * BLOCK_BYTES)
-            nc.scalar.dma_start(raw[:], h_rows[:, :, b * P : (b + 1) * P])
-            raws.append(raw)
-            if b == 1:
-                norm_rows = late.tile([P, U], F32, name="norm_rows", offset=BLOCK_BYTES)
-                nc.scalar.dma_start(norm_rows[:], norm)
+        zeros = keep.tile([P, LATER_WINDOW - U], F32, name="zeros", tag="words")
+        nc.vector.memset(zeros[:], 0.0)
+        store_scales = late.tile([P, T], U8, name="store_scales", offset=BLOCK_BYTES - 32)
+        nc.vector.memset(store_scales[:].bitcast(U32), 0)
+        nc.scalar.dma_start(store_scales[32:96:4, :].bitcast(I32), x_scales[0].bitcast(I32))
+        nc.vector.tensor_copy(windows[1][:, U:], zeros[:])
+        store_words = keep.tile([P, T], U32, name="store_words", tag="words")
+        nc.scalar.dma_start(
+            store_words[:].bitcast(I32), x_words[0].rearrange("p n t -> p (n t)").bitcast(I32)
+        )
 
         picked_scales = keep.tile([P, S], U8, name="picked_scales", align_bytes=64)
         nc.vector.memset(picked_scales[:].bitcast(I32), 0)
         nc.vector.memset(windows[0][:, R:], 0.0)
-        for d in (1, 2):
-            nc.vector.memset(windows[d][:, R:U], 0.0)
-        nc.vector.memset(windows[3][:, R:], 0.0)
+        nc.vector.memset(windows[1][:, R:U], 0.0)
+        for d in (2, 3):
+            nc.vector.memset(windows[d][:, R:], 0.0)
 
         spread_scales = keep.tile([P, S], U8, name="spread_scales")
         nc.vector.tensor_copy(spread_scales[:], store_scales[:].indirect(picks[:]))
@@ -86,7 +74,14 @@ def tile_picked_yadc_dist_p_kernel(
                 spread_scales[32 + 4 * r : 96 : 16, :].bitcast(I32),
             )
 
-        picked_words = head.tile([P, S], U32, name="picked_words", offset=0, align_bytes=64)
+        raw1 = late.tile([P, PACK, P], F32, name="raw1", offset=0)
+        nc.sync.dma_start(raw1[:], h_rows[:, :, P : 2 * P])
+        norm_rows = late.tile([P, U], F32, name="norm_rows", offset=BLOCK_BYTES)
+        nc.sync.dma_start(norm_rows[:], norm)
+        raw23 = late.tile([P, PACK, 2 * P], F32, name="raw23", offset=2 * BLOCK_BYTES)
+        nc.sync.dma_start(raw23[:], h_rows[:, :, 2 * P :])
+        raws = [raw0[:], raw1[:], raw23[:, :, :P], raw23[:, :, P:]]
+
         h_codes = keep.tile([P, V], U32, name="h_codes", align_bytes=64)
         h_scales = keep.tile([P, V], U8, name="h_scales", align_bytes=64)
 
@@ -97,18 +92,11 @@ def tile_picked_yadc_dist_p_kernel(
             )
 
         def prepare(b):
-            copy = nc.vector.tensor_copy if b == 0 else nc.scalar.copy
-            if b < 2:
-                grouped = head.tile(
-                    [P, P, PACK], BF16, name="grouped%d" % b, offset=T - 512 + 512 * b, align_bytes=64
-                )
-            else:
-                grouped = keep.tile(
-                    [P, P, PACK], BF16, name="grouped%d" % b, tag="sum0_%d" % (b - 2), align_bytes=64
-                )
-            copy(
+            tag = ("picked", "grouped1", "sum0_0", "sum0_1")[b]
+            grouped = keep.tile([P, P, PACK], BF16, name="grouped%d" % b, tag=tag, align_bytes=64)
+            nc.scalar.copy(
                 grouped[:].rearrange("p (c i) j -> p c j i", i=4),
-                raws[b][:].rearrange("p j (c i) -> p c j i", i=4),
+                raws[b].rearrange("p j (c i) -> p c j i", i=4),
             )
             nc.vector.quantize_mx(
                 out=h_codes[:, b * P : (b + 1) * P].bitcast(FP8X4),
@@ -144,6 +132,7 @@ def tile_picked_yadc_dist_p_kernel(
                     nc.sync.dma_start(out[b * P : (b + 1) * P, cols], sums[b, d][:, cols])
 
         prepare(0)
+        picked_words = keep.tile([P, S], U32, name="picked_words", tag="picked", align_bytes=64)
         pick_words(0)
         pick_words(1)
         prepare(1)

@@ -107,7 +107,7 @@ def tile_picked_yadc_dist_p_kernel(
         sums = {}
 
         def look_up(b, d, pieces):
-            bank = psum.tile([P, R], F32, name="bank")
+            bank = psum.tile([P, R], F32, name="bank", tag="bank%d" % (len(sums) % 2))
             nc.tensor.matmul_mx(
                 out=bank[:],
                 lhsT=h_codes[:, b * P : (b + 1) * P].bitcast(FP8X4),

@@ -33,13 +33,14 @@ def tile_picked_yadc_dist_p_kernel(
     with ExitStack() as ctx:
         keep = ctx.enter_context(tc.tile_pool(name="keep", bufs=1))
         late = ctx.enter_context(tc.tile_pool(name="late", bufs=1))
+        early = ctx.enter_context(tc.tile_pool(name="early", bufs=1))
         psum = ctx.enter_context(tc.psum_pool(name="psum", bufs=1))
 
         picks = keep.tile([P, S // LIST_ROWS], U16, name="picks")
         nc.sync.dma_start(picks[:], offs)
         h_rows = hT.rearrange("(p j) t -> p j t", j=PACK)
         raw0 = keep.tile([P, PACK, P], F32, name="raw0")
-        nc.scalar.dma_start(raw0[:], h_rows[:, :, :P])
+        nc.sync.dma_start(raw0[:], h_rows[:, :, :P])
         codes = [keep.tile([P, U // LIST_ROWS], U16, name="code%d" % d) for d in range(BOOKS)]
         for tile, code in zip(codes, (code1, code2, code3, code4)):
             nc.sync.dma_start(tile[:], code)
@@ -48,23 +49,30 @@ def tile_picked_yadc_dist_p_kernel(
             keep.tile([P, FIRST_WINDOW if d == 0 else LATER_WINDOW], F32, name="table%d" % d)
             for d in range(BOOKS)
         ]
-        zeros = keep.tile([P, LATER_WINDOW - U], F32, name="zeros", tag="words")
+        zeros = early.tile([P, LATER_WINDOW - U], F32, name="zeros", offset=4 * T - 32)
         nc.vector.memset(zeros[:], 0.0)
-        store_scales = late.tile([P, T], U8, name="store_scales", offset=BLOCK_BYTES - 32)
+        store_scales = late.tile([P, T], U8, name="store_scales", offset=4096)
         nc.vector.memset(store_scales[:].bitcast(U32), 0)
-        nc.scalar.dma_start(store_scales[32:96:4, :].bitcast(I32), x_scales[0].bitcast(I32))
+        nc.sync.dma_start(store_scales[32:96:4, :].bitcast(I32), x_scales[0].bitcast(I32))
         nc.vector.tensor_copy(windows[1][:, U:], zeros[:])
-        store_words = keep.tile([P, T], U32, name="store_words", tag="words")
-        nc.scalar.dma_start(
+        store_words = early.tile([P, T], U32, name="store_words", offset=0)
+        nc.sync.dma_start(
             store_words[:].bitcast(I32), x_words[0].rearrange("p n t -> p (n t)").bitcast(I32)
         )
+        raw1 = early.tile([P, PACK, P], F32, name="raw1", offset=4 * T)
+        nc.sync.dma_start(raw1[:], h_rows[:, :, P : 2 * P])
 
         picked_scales = keep.tile([P, S], U8, name="picked_scales", align_bytes=64)
         nc.vector.memset(picked_scales[:].bitcast(I32), 0)
+        first_table = keep.tile([P, U], F32, name="first_table")
+        nc.vector.memset(first_table[:, R:], 0.0)
         nc.vector.memset(windows[0][:, R:], 0.0)
         nc.vector.memset(windows[1][:, R:U], 0.0)
         for d in (2, 3):
             nc.vector.memset(windows[d][:, R:], 0.0)
+
+        last_table = keep.tile([P, R + 16], F32, name="last_table")
+        nc.vector.memset(last_table[:, R:], 0.0)
 
         spread_scales = keep.tile([P, S], U8, name="spread_scales")
         nc.vector.tensor_copy(spread_scales[:], store_scales[:].indirect(picks[:]))
@@ -74,11 +82,9 @@ def tile_picked_yadc_dist_p_kernel(
                 spread_scales[32 + 4 * r : 96 : 16, :].bitcast(I32),
             )
 
-        raw1 = late.tile([P, PACK, P], F32, name="raw1", offset=0)
-        nc.sync.dma_start(raw1[:], h_rows[:, :, P : 2 * P])
-        norm_rows = late.tile([P, U], F32, name="norm_rows", offset=BLOCK_BYTES)
+        norm_rows = late.tile([P, U], F32, name="norm_rows", offset=4608)
         nc.sync.dma_start(norm_rows[:], norm)
-        raw23 = late.tile([P, PACK, 2 * P], F32, name="raw23", offset=2 * BLOCK_BYTES)
+        raw23 = late.tile([P, PACK, 2 * P], F32, name="raw23", offset=4608 + BLOCK_BYTES)
         nc.sync.dma_start(raw23[:], h_rows[:, :, 2 * P :])
         raws = [raw0[:], raw1[:], raw23[:, :, :P], raw23[:, :, P:]]
 
@@ -93,8 +99,12 @@ def tile_picked_yadc_dist_p_kernel(
 
         def prepare(b):
             tag = ("picked", "grouped1", "sum0_0", "sum0_1")[b]
-            grouped = keep.tile([P, P, PACK], BF16, name="grouped%d" % b, tag=tag, align_bytes=64)
-            nc.scalar.copy(
+            if b == 0:
+                grouped = late.tile([P, P, PACK], BF16, name="grouped0", offset=3584, align_bytes=64)
+            else:
+                grouped = keep.tile([P, P, PACK], BF16, name="grouped%d" % b, tag=tag, align_bytes=64)
+            copy = nc.vector.tensor_copy if b == 0 else nc.scalar.copy
+            copy(
                 grouped[:].rearrange("p (c i) j -> p c j i", i=4),
                 raws[b].rearrange("p j (c i) -> p c j i", i=4),
             )
@@ -107,7 +117,7 @@ def tile_picked_yadc_dist_p_kernel(
         sums = {}
 
         def look_up(b, d, pieces):
-            bank = psum.tile([P, R], F32, name="bank", tag="bank%d" % (len(sums) % 2))
+            bank = psum.tile([P, R], F32, name="bank", tag="bank%d" % (len(sums) // 2 % 2 if sums else 2))
             nc.tensor.matmul_mx(
                 out=bank[:],
                 lhsT=h_codes[:, b * P : (b + 1) * P].bitcast(FP8X4),
@@ -117,13 +127,14 @@ def tile_picked_yadc_dist_p_kernel(
                 start=True,
                 stop=True,
             )
-            nc.scalar.copy(windows[d][:, :R], bank[:])
+            table = {(0, 0): first_table, (BLOCKS - 1, BOOKS - 1): last_table}.get((b, d), windows[d])
+            nc.scalar.copy(table[:, :R], bank[:])
             sums[b, d] = keep.tile([P, U], F32, name="sum%d_%d" % (b, d), tag="sum%d_%d" % (b, d), align_bytes=64)
             width = U // pieces
             for i in range(pieces):
                 cols = slice(i * width, (i + 1) * width)
                 offsets = codes[d][:, i * width // LIST_ROWS : (i + 1) * width // LIST_ROWS]
-                entries = windows[d][:].indirect(offsets)
+                entries = table[:].indirect(offsets)
                 if d == 0:
                     nc.vector.tensor_tensor(sums[b, d][:, cols], entries, norm_rows[:, cols], SUBTRACT)
                 else:
@@ -132,7 +143,7 @@ def tile_picked_yadc_dist_p_kernel(
                     nc.sync.dma_start(out[b * P : (b + 1) * P, cols], sums[b, d][:, cols])
 
         prepare(0)
-        picked_words = keep.tile([P, S], U32, name="picked_words", tag="picked", align_bytes=64)
+        picked_words = late.tile([P, S], U32, name="picked_words", offset=0, align_bytes=64)
         pick_words(0)
         pick_words(1)
         prepare(1)

@@ -24,6 +24,8 @@ BLOCKS = V // P
 FIRST_WINDOW = 2 * U
 LATER_WINDOW = U + 16
 BLOCK_BYTES = PACK * P * 4
+VECTOR_SHARE = 520
+LAST_CUT = 352
 
 
 def tile_picked_yadc_dist_p_kernel(
@@ -41,8 +43,9 @@ def tile_picked_yadc_dist_p_kernel(
         h_rows = hT.rearrange("(p j) t -> p j t", j=PACK)
         raw0 = keep.tile([P, PACK, P], F32, name="raw0")
         nc.sync.dma_start(raw0[:], h_rows[:, :, :P])
+
         codes = [keep.tile([P, U // LIST_ROWS], U16, name="code%d" % d) for d in range(BOOKS)]
-        for tile, code in zip(codes, (code1, code2, code3, code4)):
+        for tile, code in zip(codes[:2], (code1, code2)):
             nc.sync.dma_start(tile[:], code)
 
         windows = [
@@ -52,7 +55,9 @@ def tile_picked_yadc_dist_p_kernel(
         zeros = early.tile([P, LATER_WINDOW - U], F32, name="zeros", offset=4 * T - 32)
         nc.vector.memset(zeros[:], 0.0)
         store_scales = late.tile([P, T], U8, name="store_scales", offset=4096)
-        nc.vector.memset(store_scales[:].bitcast(U32), 0)
+        cleared = store_scales[:].bitcast(U32)
+        nc.vector.memset(cleared[:, :VECTOR_SHARE], 0)
+        nc.gpsimd.memset(cleared[:, VECTOR_SHARE:], 0)
         nc.sync.dma_start(store_scales[32:96:4, :].bitcast(I32), x_scales[0].bitcast(I32))
         nc.vector.tensor_copy(windows[1][:, U:], zeros[:])
         store_words = early.tile([P, T], U32, name="store_words", offset=0)
@@ -61,6 +66,9 @@ def tile_picked_yadc_dist_p_kernel(
         )
         raw1 = early.tile([P, PACK, P], F32, name="raw1", offset=4 * T)
         nc.sync.dma_start(raw1[:], h_rows[:, :, P : 2 * P])
+
+        for tile, code in zip(codes[2:], (code3, code4)):
+            nc.sync.dma_start(tile[:], code)
 
         picked_scales = keep.tile([P, S], U8, name="picked_scales", align_bytes=64)
         nc.vector.memset(picked_scales[:].bitcast(I32), 0)
@@ -71,7 +79,7 @@ def tile_picked_yadc_dist_p_kernel(
         for d in (2, 3):
             nc.vector.memset(windows[d][:, R:], 0.0)
 
-        last_table = keep.tile([P, R + 16], F32, name="last_table")
+        last_table = keep.tile([P, LAST_CUT + 16], F32, name="last_table")
         nc.vector.memset(last_table[:, R:], 0.0)
 
         spread_scales = keep.tile([P, S], U8, name="spread_scales")
@@ -130,10 +138,9 @@ def tile_picked_yadc_dist_p_kernel(
             table = {(0, 0): first_table, (BLOCKS - 1, BOOKS - 1): last_table}.get((b, d), windows[d])
             nc.scalar.copy(table[:, :R], bank[:])
             sums[b, d] = keep.tile([P, U], F32, name="sum%d_%d" % (b, d), tag="sum%d_%d" % (b, d), align_bytes=64)
-            width = U // pieces
-            for i in range(pieces):
-                cols = slice(i * width, (i + 1) * width)
-                offsets = codes[d][:, i * width // LIST_ROWS : (i + 1) * width // LIST_ROWS]
+            for lo, hi in pieces:
+                cols = slice(lo, hi)
+                offsets = codes[d][:, lo // LIST_ROWS : hi // LIST_ROWS]
                 entries = table[:].indirect(offsets)
                 if d == 0:
                     nc.vector.tensor_tensor(sums[b, d][:, cols], entries, norm_rows[:, cols], SUBTRACT)
@@ -150,6 +157,7 @@ def tile_picked_yadc_dist_p_kernel(
         order = [(0, 0), (0, 1), (1, 0), (0, 2), (1, 1), (0, 3), (1, 2), (2, 0),
                  (1, 3), (2, 1), (3, 0), (2, 2), (3, 1), (2, 3), (3, 2), (3, 3)]
         for i, (b, d) in enumerate(order):
-            look_up(b, d, 2 if i < 2 or i >= len(order) - 2 else 1)
+            cut = U // 2 if i < 2 else LAST_CUT if i >= len(order) - 2 else U
+            look_up(b, d, [(lo, hi) for lo, hi in ((0, cut), (cut, U)) if lo < hi])
             if b == 0 and d in (1, 2):
                 prepare(d + 1)

@@ -56,7 +56,8 @@ def tile_picked_yadc_dist_p_kernel(
         nc.vector.memset(zeros[:], 0.0)
         store_scales = late.tile([P, T], U8, name="store_scales", offset=4096)
         cleared = store_scales[:].bitcast(U32)
-        nc.vector.memset(cleared[:, :VECTOR_SHARE], 0)
+        nc.vector.memset(cleared[:, : VECTOR_SHARE - 7], 0)
+        nc.vector.memset(cleared[:, VECTOR_SHARE - 7 : VECTOR_SHARE], 0)
         nc.gpsimd.memset(cleared[:, VECTOR_SHARE:], 0)
         nc.sync.dma_start(store_scales[32:96:4, :].bitcast(I32), x_scales[0].bitcast(I32))
         nc.vector.tensor_copy(windows[1][:, U:], zeros[:])
@@ -125,18 +126,20 @@ def tile_picked_yadc_dist_p_kernel(
         sums = {}
 
         def look_up(b, d, pieces):
-            bank = psum.tile([P, R], F32, name="bank", tag="bank%d" % (len(sums) // 2 % 2 if sums else 2))
-            nc.tensor.matmul_mx(
-                out=bank[:],
-                lhsT=h_codes[:, b * P : (b + 1) * P].bitcast(FP8X4),
-                lhsT_scale=h_scales[:, b * P : (b + 1) * P],
-                rhs=picked_words[:, d * R : (d + 1) * R].bitcast(FP8X4),
-                rhs_scale=picked_scales[:, d * R : (d + 1) * R],
-                start=True,
-                stop=True,
-            )
             table = {(0, 0): first_table, (BLOCKS - 1, BOOKS - 1): last_table}.get((b, d), windows[d])
-            nc.scalar.copy(table[:, :R], bank[:])
+            parts = [(len(sums) // 2 % 2, 0, R)] if sums else [(2, 0, R // 2), (3, R // 2, R)]
+            for turn, lo, hi in parts:
+                bank = psum.tile([P, hi - lo], F32, name="bank", tag="bank%d" % turn)
+                nc.tensor.matmul_mx(
+                    out=bank[:],
+                    lhsT=h_codes[:, b * P : (b + 1) * P].bitcast(FP8X4),
+                    lhsT_scale=h_scales[:, b * P : (b + 1) * P],
+                    rhs=picked_words[:, d * R + lo : d * R + hi].bitcast(FP8X4),
+                    rhs_scale=picked_scales[:, d * R + lo : d * R + hi],
+                    start=True,
+                    stop=True,
+                )
+                nc.scalar.copy(table[:, lo:hi], bank[:])
             sums[b, d] = keep.tile([P, U], F32, name="sum%d_%d" % (b, d), tag="sum%d_%d" % (b, d), align_bytes=64)
             for lo, hi in pieces:
                 cols = slice(lo, hi)

@@ -62,9 +62,9 @@ def tile_picked_yadc_dist_p_kernel(
         nc.sync.dma_start(store_scales[32:96:4, :].bitcast(I32), x_scales[0].bitcast(I32))
         nc.vector.tensor_copy(windows[1][:, U:], zeros[:])
         store_words = early.tile([P, T], U32, name="store_words", offset=0)
-        nc.sync.dma_start(
-            store_words[:].bitcast(I32), x_words[0].rearrange("p n t -> p (n t)").bitcast(I32)
-        )
+        word_rows = x_words[0].rearrange("p n t -> p (n t)").bitcast(I32)
+        for lo in range(0, T, T // 2):
+            nc.sync.dma_start(store_words[:, lo : lo + T // 2].bitcast(I32), word_rows[:, lo : lo + T // 2])
         raw1 = early.tile([P, PACK, P], F32, name="raw1", offset=4 * T)
         nc.sync.dma_start(raw1[:], h_rows[:, :, P : 2 * P])
 

@@ -1,6 +1,7 @@
 from contextlib import ExitStack
 
 import concourse.mybir as mybir
+from concourse.masks import make_identity
 
 K, T, S, V, U, R = 512, 4096, 1024, 512, 512, 256
 BOOKS = 4
@@ -15,17 +16,19 @@ U8 = mybir.dt.uint8
 FP8X4 = mybir.dt.float8_e4m3fn_x4
 ADD = mybir.AluOpType.add
 SUBTRACT = mybir.AluOpType.subtract
+COPY = mybir.ActivationFunctionType.Copy
 
 P = 128
 PACK = 4
 LIST_ROWS = 16
 HALF = S // 2
 BLOCKS = V // P
-FIRST_WINDOW = 2 * U
-LATER_WINDOW = U + 16
+VECTOR_COLS = (384, 256, 256, 384)
+FIRST_WINDOW = 2 * max(VECTOR_COLS)
+LATER_WINDOW = max(VECTOR_COLS) + 16
 BLOCK_BYTES = PACK * P * 4
 VECTOR_SHARE = 520
-LAST_CUT = 352
+PRODUCT_BANKS = 4
 
 
 def tile_picked_yadc_dist_p_kernel(
@@ -48,11 +51,12 @@ def tile_picked_yadc_dist_p_kernel(
         for tile, code in zip(codes[:2], (code1, code2)):
             nc.sync.dma_start(tile[:], code)
 
-        windows = [
-            keep.tile([P, FIRST_WINDOW if d == 0 else LATER_WINDOW], F32, name="table%d" % d)
+        windows = {
+            (s, d): keep.tile([P, FIRST_WINDOW if d == 0 else LATER_WINDOW], F32, name="table%d_%d" % (s, d))
+            for s in range(2)
             for d in range(BOOKS)
-        ]
-        zeros = early.tile([P, LATER_WINDOW - U], F32, name="zeros", offset=4 * T - 32)
+        }
+        zeros = early.tile([P, 16], F32, name="zeros", offset=4 * T - 32)
         nc.vector.memset(zeros[:], 0.0)
         store_scales = late.tile([P, T], U8, name="store_scales", offset=4096)
         cleared = store_scales[:].bitcast(U32)
@@ -60,7 +64,7 @@ def tile_picked_yadc_dist_p_kernel(
         nc.vector.memset(cleared[:, VECTOR_SHARE - 7 : VECTOR_SHARE], 0)
         nc.gpsimd.memset(cleared[:, VECTOR_SHARE:], 0)
         nc.sync.dma_start(store_scales[32:96:4, :].bitcast(I32), x_scales[0].bitcast(I32))
-        nc.vector.tensor_copy(windows[1][:, U:], zeros[:])
+        nc.vector.tensor_copy(windows[0, 1][:, LATER_WINDOW - 16 :], zeros[:])
         store_words = early.tile([P, T], U32, name="store_words", offset=0)
         word_rows = x_words[0].rearrange("p n t -> p (n t)").bitcast(I32)
         for lo in range(0, T, T // 2):
@@ -73,15 +77,10 @@ def tile_picked_yadc_dist_p_kernel(
 
         picked_scales = keep.tile([P, S], U8, name="picked_scales", align_bytes=64)
         nc.vector.memset(picked_scales[:].bitcast(I32), 0)
-        first_table = keep.tile([P, U], F32, name="first_table")
-        nc.vector.memset(first_table[:, R:], 0.0)
-        nc.vector.memset(windows[0][:, R:], 0.0)
-        nc.vector.memset(windows[1][:, R:U], 0.0)
-        for d in (2, 3):
-            nc.vector.memset(windows[d][:, R:], 0.0)
-
-        last_table = keep.tile([P, LAST_CUT + 16], F32, name="last_table")
-        nc.vector.memset(last_table[:, R:], 0.0)
+        for key, table in windows.items():
+            nc.vector.memset(table[:, R : LATER_WINDOW - 16] if key == (0, 1) else table[:, R:], 0.0)
+        identity = keep.tile([P, P], F32, name="identity")
+        make_identity(nc, identity[:])
 
         spread_scales = keep.tile([P, S], U8, name="spread_scales")
         nc.vector.tensor_copy(spread_scales[:], store_scales[:].indirect(picks[:]))
@@ -112,7 +111,7 @@ def tile_picked_yadc_dist_p_kernel(
                 grouped = late.tile([P, P, PACK], BF16, name="grouped0", offset=3584, align_bytes=64)
             else:
                 grouped = keep.tile([P, P, PACK], BF16, name="grouped%d" % b, tag=tag, align_bytes=64)
-            copy = nc.vector.tensor_copy if b == 0 else nc.scalar.copy
+            copy = nc.vector.tensor_copy if b in (0, 3) else nc.scalar.copy
             copy(
                 grouped[:].rearrange("p (c i) j -> p c j i", i=4),
                 raws[b].rearrange("p j (c i) -> p c j i", i=4),
@@ -123,44 +122,99 @@ def tile_picked_yadc_dist_p_kernel(
                 in_=grouped[:].rearrange("p t j -> p (t j)"),
             )
 
-        sums = {}
+        order = [(0, 0), (0, 1), (1, 0), (0, 2), (1, 1), (0, 3), (1, 2), (2, 0),
+                 (1, 3), (2, 1), (3, 0), (2, 2), (3, 1), (2, 3), (3, 2), (3, 3)]
+        banks, sums, turned, backs = {}, {}, {}, {}
 
-        def look_up(b, d, pieces):
-            table = {(0, 0): first_table, (BLOCKS - 1, BOOKS - 1): last_table}.get((b, d), windows[d])
-            parts = [(len(sums) // 2 % 2, 0, R)] if sums else [(2, 0, R // 2), (3, R // 2, R)]
-            for turn, lo, hi in parts:
-                bank = psum.tile([P, hi - lo], F32, name="bank", tag="bank%d" % turn)
-                nc.tensor.matmul_mx(
-                    out=bank[:],
-                    lhsT=h_codes[:, b * P : (b + 1) * P].bitcast(FP8X4),
-                    lhsT_scale=h_scales[:, b * P : (b + 1) * P],
-                    rhs=picked_words[:, d * R + lo : d * R + hi].bitcast(FP8X4),
-                    rhs_scale=picked_scales[:, d * R + lo : d * R + hi],
-                    start=True,
-                    stop=True,
-                )
-                nc.scalar.copy(table[:, lo:hi], bank[:])
+        def multiply(i):
+            b, d = order[i]
+            banks[i] = psum.tile([P, R], F32, name="bank", tag="bank%d" % (i % PRODUCT_BANKS))
+            nc.tensor.matmul_mx(
+                out=banks[i][:],
+                lhsT=h_codes[:, b * P : (b + 1) * P].bitcast(FP8X4),
+                lhsT_scale=h_scales[:, b * P : (b + 1) * P],
+                rhs=picked_words[:, d * R : (d + 1) * R].bitcast(FP8X4),
+                rhs_scale=picked_scales[:, d * R : (d + 1) * R],
+                start=True,
+                stop=True,
+            )
+
+        def fill(i):
+            b, d = order[i]
+            nc.scalar.copy(windows[b % 2, d][:, :R], banks[i][:])
+
+        def entries(b, d, lo, hi):
+            return windows[b % 2, d][:].indirect(codes[d][:, lo // LIST_ROWS : hi // LIST_ROWS])
+
+        def vector_look_up(i):
+            b, d = order[i]
+            width = VECTOR_COLS[b]
             sums[b, d] = keep.tile([P, U], F32, name="sum%d_%d" % (b, d), tag="sum%d_%d" % (b, d), align_bytes=64)
-            for lo, hi in pieces:
-                cols = slice(lo, hi)
-                offsets = codes[d][:, lo // LIST_ROWS : hi // LIST_ROWS]
-                entries = table[:].indirect(offsets)
-                if d == 0:
-                    nc.vector.tensor_tensor(sums[b, d][:, cols], entries, norm_rows[:, cols], SUBTRACT)
-                else:
-                    nc.vector.tensor_tensor(sums[b, d][:, cols], entries, sums[b, d - 1][:, cols], ADD)
-                if d == BOOKS - 1:
-                    nc.sync.dma_start(out[b * P : (b + 1) * P, cols], sums[b, d][:, cols])
+            cut = width // 2 if i < 2 else 256 if i >= len(order) - 2 else width
+            for lo, hi in ((0, cut), (cut, width)):
+                if lo < hi:
+                    cols = slice(lo, hi)
+                    if d == 0:
+                        nc.vector.tensor_tensor(sums[b, d][:, cols], entries(b, d, lo, hi), norm_rows[:, cols], SUBTRACT)
+                    else:
+                        nc.vector.tensor_tensor(sums[b, d][:, cols], entries(b, d, lo, hi), sums[b, d - 1][:, cols], ADD)
+                    if d == BOOKS - 1:
+                        nc.sync.dma_start(out[b * P : (b + 1) * P, cols], sums[b, d][:, cols])
+
+        def scalar_look_up(i):
+            b, d = order[i]
+            lo = VECTOR_COLS[b]
+            width = U - lo
+            found = keep.tile([P, width], F32, name="found%d_%d" % (b, d))
+            nc.scalar.activation(found[:], entries(b, d, lo, U), COPY)
+            if d == 0:
+                turned[b] = psum.tile([P, width], F32, name="turned", tag="turned%d" % (b % 2))
+            for c in range(0, width, P):
+                nc.tensor.matmul(
+                    turned[b][:, c : c + P],
+                    found[:, c : c + P],
+                    identity[:],
+                    is_transpose=True,
+                    start=(d == 0 and c == 0),
+                    stop=(d == BOOKS - 1 and c == width - P),
+                )
+
+        def turn_back(b):
+            width = U - VECTOR_COLS[b]
+            middle = keep.tile([P, width], F32, name="middle%d" % b)
+            nc.scalar.copy(middle[:], turned[b][:])
+            backs[b] = psum.tile([P, width], F32, name="back", tag="back%d" % (b % 2))
+            for c in range(0, width, P):
+                nc.tensor.transpose(backs[b][:, c : c + P], middle[:, c : c + P], identity[:])
+
+        def finish(b):
+            lo = VECTOR_COLS[b]
+            result = keep.tile([P, U - lo], F32, name="result%d" % b)
+            nc.vector.tensor_tensor(result[:], backs[b][:], norm_rows[:, lo:], SUBTRACT)
+            nc.sync.dma_start(out[b * P : (b + 1) * P, lo:], result[:])
 
         prepare(0)
         picked_words = late.tile([P, S], U32, name="picked_words", offset=0, align_bytes=64)
         pick_words(0)
         pick_words(1)
         prepare(1)
-        order = [(0, 0), (0, 1), (1, 0), (0, 2), (1, 1), (0, 3), (1, 2), (2, 0),
-                 (1, 3), (2, 1), (3, 0), (2, 2), (3, 1), (2, 3), (3, 2), (3, 3)]
+        steps = len(order)
+        for i in range(3):
+            multiply(i)
+        for i in range(2):
+            fill(i)
         for i, (b, d) in enumerate(order):
-            cut = U // 2 if i < 2 else LAST_CUT if i >= len(order) - 2 else U
-            look_up(b, d, [(lo, hi) for lo, hi in ((0, cut), (cut, U)) if lo < hi])
+            if i + 3 < steps:
+                multiply(i + 3)
+            if i + 2 < steps:
+                fill(i + 2)
+            scalar_look_up(i)
+            if i >= 1 and order[i - 1][1] == BOOKS - 1:
+                turn_back(order[i - 1][0])
+            vector_look_up(i)
+            if i >= 2 and order[i - 2][1] == BOOKS - 1:
+                finish(order[i - 2][0])
             if b == 0 and d in (1, 2):
                 prepare(d + 1)
+        turn_back(BLOCKS - 1)
+        finish(BLOCKS - 1)

@@ -23,12 +23,12 @@ PACK = 4
 LIST_ROWS = 16
 HALF = S // 2
 BLOCKS = V // P
-VECTOR_COLS = (384, 256, 256, 384)
-FIRST_WINDOW = 2 * max(VECTOR_COLS)
-LATER_WINDOW = max(VECTOR_COLS) + 16
+VECTOR_COLS = (256, 512, 0, 512)
+SPARE = 16
 BLOCK_BYTES = PACK * P * 4
 VECTOR_SHARE = 520
 PRODUCT_BANKS = 4
+LAST_CUT = 352
 
 
 def tile_picked_yadc_dist_p_kernel(
@@ -51,12 +51,16 @@ def tile_picked_yadc_dist_p_kernel(
         for tile, code in zip(codes[:2], (code1, code2)):
             nc.sync.dma_start(tile[:], code)
 
+        def window_width(b, d):
+            longest = max(VECTOR_COLS[b], U - VECTOR_COLS[b])
+            return 2 * longest if d == 0 and VECTOR_COLS[b] else longest + SPARE
+
         windows = {
-            (s, d): keep.tile([P, FIRST_WINDOW if d == 0 else LATER_WINDOW], F32, name="table%d_%d" % (s, d))
-            for s in range(2)
+            (b, d): keep.tile([P, window_width(b, d)], F32, name="table%d_%d" % (b, d))
+            for b in range(BLOCKS)
             for d in range(BOOKS)
         }
-        zeros = early.tile([P, 16], F32, name="zeros", offset=4 * T - 32)
+        zeros = early.tile([P, SPARE], F32, name="zeros", offset=4 * T - 32)
         nc.vector.memset(zeros[:], 0.0)
         store_scales = late.tile([P, T], U8, name="store_scales", offset=4096)
         cleared = store_scales[:].bitcast(U32)
@@ -64,7 +68,7 @@ def tile_picked_yadc_dist_p_kernel(
         nc.vector.memset(cleared[:, VECTOR_SHARE - 7 : VECTOR_SHARE], 0)
         nc.gpsimd.memset(cleared[:, VECTOR_SHARE:], 0)
         nc.sync.dma_start(store_scales[32:96:4, :].bitcast(I32), x_scales[0].bitcast(I32))
-        nc.vector.tensor_copy(windows[0, 1][:, LATER_WINDOW - 16 :], zeros[:])
+        nc.vector.tensor_copy(windows[0, 1][:, R:], zeros[:])
         store_words = early.tile([P, T], U32, name="store_words", offset=0)
         word_rows = x_words[0].rearrange("p n t -> p (n t)").bitcast(I32)
         for lo in range(0, T, T // 2):
@@ -77,8 +81,10 @@ def tile_picked_yadc_dist_p_kernel(
 
         picked_scales = keep.tile([P, S], U8, name="picked_scales", align_bytes=64)
         nc.vector.memset(picked_scales[:].bitcast(I32), 0)
+        nc.vector.memset(windows[1, 0][:, R:], 0.0)
         for key, table in windows.items():
-            nc.vector.memset(table[:, R : LATER_WINDOW - 16] if key == (0, 1) else table[:, R:], 0.0)
+            if key not in ((0, 1), (1, 0)):
+                nc.scalar.copy(table[:, R:], windows[1, 0][:, R : window_width(*key)])
         identity = keep.tile([P, P], F32, name="identity")
         make_identity(nc, identity[:])
 
@@ -94,7 +100,8 @@ def tile_picked_yadc_dist_p_kernel(
         nc.sync.dma_start(norm_rows[:], norm)
         raw23 = late.tile([P, PACK, 2 * P], F32, name="raw23", offset=4608 + BLOCK_BYTES)
         nc.sync.dma_start(raw23[:], h_rows[:, :, 2 * P :])
-        raws = [raw0[:], raw1[:], raw23[:, :, :P], raw23[:, :, P:]]
+        raws = [raw0[:], raw1[:], raw23[:]]
+        widths = [P, P, 2 * P]
 
         h_codes = keep.tile([P, V], U32, name="h_codes", align_bytes=64)
         h_scales = keep.tile([P, V], U8, name="h_scales", align_bytes=64)
@@ -105,32 +112,29 @@ def tile_picked_yadc_dist_p_kernel(
                 picked_words[:, h * HALF : (h + 1) * HALF], store_words[:].indirect(picks[:, h * cols : (h + 1) * cols])
             )
 
-        def prepare(b):
-            tag = ("picked", "grouped1", "sum0_0", "sum0_1")[b]
+        grouped, banks, sums, turned, backs = {}, {}, {}, {}, {}
+
+        def interleave(b, copy, tag=None):
             if b == 0:
-                grouped = late.tile([P, P, PACK], BF16, name="grouped0", offset=3584, align_bytes=64)
+                grouped[b] = late.tile([P, P, PACK], BF16, name="grouped0", offset=3584, align_bytes=64)
             else:
-                grouped = keep.tile([P, P, PACK], BF16, name="grouped%d" % b, tag=tag, align_bytes=64)
-            copy = nc.vector.tensor_copy if b in (0, 3) else nc.scalar.copy
+                grouped[b] = keep.tile([P, widths[b], PACK], BF16, name="grouped%d" % b, tag=tag or "grouped%d" % b, align_bytes=64)
             copy(
-                grouped[:].rearrange("p (c i) j -> p c j i", i=4),
+                grouped[b][:].rearrange("p (c i) j -> p c j i", i=4),
                 raws[b].rearrange("p j (c i) -> p c j i", i=4),
             )
+
+        def quantise(b):
             nc.vector.quantize_mx(
-                out=h_codes[:, b * P : (b + 1) * P].bitcast(FP8X4),
-                scales=h_scales[:, b * P : (b + 1) * P],
-                in_=grouped[:].rearrange("p t j -> p (t j)"),
+                out=h_codes[:, b * P : b * P + widths[b]].bitcast(FP8X4),
+                scales=h_scales[:, b * P : b * P + widths[b]],
+                in_=grouped[b][:].rearrange("p t j -> p (t j)"),
             )
 
-        order = [(0, 0), (0, 1), (1, 0), (0, 2), (1, 1), (0, 3), (1, 2), (2, 0),
-                 (1, 3), (2, 1), (3, 0), (2, 2), (3, 1), (2, 3), (3, 2), (3, 3)]
-        banks, sums, turned, backs = {}, {}, {}, {}
-
-        def multiply(i):
-            b, d = order[i]
-            banks[i] = psum.tile([P, R], F32, name="bank", tag="bank%d" % (i % PRODUCT_BANKS))
+        def multiply(b, d):
+            banks[b, d] = psum.tile([P, R], F32, name="bank", tag="bank%d" % (len(banks) % PRODUCT_BANKS))
             nc.tensor.matmul_mx(
-                out=banks[i][:],
+                out=banks[b, d][:],
                 lhsT=h_codes[:, b * P : (b + 1) * P].bitcast(FP8X4),
                 lhsT_scale=h_scales[:, b * P : (b + 1) * P],
                 rhs=picked_words[:, d * R : (d + 1) * R].bitcast(FP8X4),
@@ -139,82 +143,157 @@ def tile_picked_yadc_dist_p_kernel(
                 stop=True,
             )
 
-        def fill(i):
-            b, d = order[i]
-            nc.scalar.copy(windows[b % 2, d][:, :R], banks[i][:])
+        def fill(b, d):
+            if VECTOR_COLS[b]:
+                nc.scalar.copy(windows[b, d][:, :R], banks[b, d][:])
+            else:
+                nc.scalar.mul(windows[b, d][:, :R], banks[b, d][:], -1.0)
 
         def entries(b, d, lo, hi):
-            return windows[b % 2, d][:].indirect(codes[d][:, lo // LIST_ROWS : hi // LIST_ROWS])
+            return windows[b, d][:].indirect(codes[d][:, lo // LIST_ROWS : hi // LIST_ROWS])
 
-        def vector_look_up(i):
-            b, d = order[i]
-            width = VECTOR_COLS[b]
-            sums[b, d] = keep.tile([P, U], F32, name="sum%d_%d" % (b, d), tag="sum%d_%d" % (b, d), align_bytes=64)
-            cut = width // 2 if i < 2 else 256 if i >= len(order) - 2 else width
-            for lo, hi in ((0, cut), (cut, width)):
-                if lo < hi:
-                    cols = slice(lo, hi)
-                    if d == 0:
-                        nc.vector.tensor_tensor(sums[b, d][:, cols], entries(b, d, lo, hi), norm_rows[:, cols], SUBTRACT)
-                    else:
-                        nc.vector.tensor_tensor(sums[b, d][:, cols], entries(b, d, lo, hi), sums[b, d - 1][:, cols], ADD)
-                    if d == BOOKS - 1:
-                        nc.sync.dma_start(out[b * P : (b + 1) * P, cols], sums[b, d][:, cols])
-
-        def scalar_look_up(i):
-            b, d = order[i]
-            lo = VECTOR_COLS[b]
-            width = U - lo
-            found = keep.tile([P, width], F32, name="found%d_%d" % (b, d))
-            nc.scalar.activation(found[:], entries(b, d, lo, U), COPY)
+        def chain(b, d, lo, hi):
+            if (b, d) not in sums:
+                sums[b, d] = keep.tile(
+                    [P, U], F32, name="sum%d_%d" % (b, d), tag="sum%d_%d" % (b, d), align_bytes=64
+                )
+            cols = slice(lo, hi)
             if d == 0:
-                turned[b] = psum.tile([P, width], F32, name="turned", tag="turned%d" % (b % 2))
-            for c in range(0, width, P):
+                nc.vector.tensor_tensor(sums[b, d][:, cols], entries(b, d, lo, hi), norm_rows[:, cols], SUBTRACT)
+            else:
+                nc.vector.tensor_tensor(sums[b, d][:, cols], entries(b, d, lo, hi), sums[b, d - 1][:, cols], ADD)
+            if d == BOOKS - 1:
+                nc.sync.dma_start(out[b * P : (b + 1) * P, cols], sums[b, d][:, cols])
+
+        found = {}
+
+        def fetch(b, d, lo, hi):
+            found[b, d, lo] = keep.tile([P, hi - lo], F32, name="found%d_%d_%d" % (b, d, lo))
+            nc.scalar.activation(found[b, d, lo][:], entries(b, d, lo, hi), COPY)
+
+        def add_turned(b, half, source, first, last):
+            if first:
+                turned[b, half] = psum.tile([P, R], F32, name="turned", tag="turned%d" % (len(turned) % 2))
+            for c in range(0, R, P):
                 nc.tensor.matmul(
-                    turned[b][:, c : c + P],
-                    found[:, c : c + P],
+                    turned[b, half][:, c : c + P],
+                    source[:, c : c + P],
                     identity[:],
                     is_transpose=True,
-                    start=(d == 0 and c == 0),
-                    stop=(d == BOOKS - 1 and c == width - P),
+                    start=(first and c == 0),
+                    stop=(last and c == R - P),
                 )
 
-        def turn_back(b):
-            width = U - VECTOR_COLS[b]
-            middle = keep.tile([P, width], F32, name="middle%d" % b)
-            nc.scalar.copy(middle[:], turned[b][:])
-            backs[b] = psum.tile([P, width], F32, name="back", tag="back%d" % (b % 2))
-            for c in range(0, width, P):
-                nc.tensor.transpose(backs[b][:, c : c + P], middle[:, c : c + P], identity[:])
+        def turn(b, d, lo, hi):
+            for at in range(lo, hi, R):
+                half = at // R
+                if d == 0 and not VECTOR_COLS[b]:
+                    add_turned(b, half, norm_rows[:, at : at + R], True, False)
+                add_turned(
+                    b, half, found[b, d, lo][:, at - lo : at - lo + R], d == 0 and VECTOR_COLS[b] > 0, d == BOOKS - 1
+                )
 
-        def finish(b):
-            lo = VECTOR_COLS[b]
-            result = keep.tile([P, U - lo], F32, name="result%d" % b)
-            nc.vector.tensor_tensor(result[:], backs[b][:], norm_rows[:, lo:], SUBTRACT)
-            nc.sync.dma_start(out[b * P : (b + 1) * P, lo:], result[:])
+        middles = {}
 
-        prepare(0)
+        def middle(b, half):
+            middles[b, half] = keep.tile([P, R], F32, name="middle%d_%d" % (b, half))
+            nc.scalar.copy(middles[b, half][:], turned[b, half][:])
+
+        def turn_back(b, half):
+            backs[b, half] = psum.tile([P, R], F32, name="back", tag="back%d" % (len(backs) % 2))
+            for c in range(0, R, P):
+                nc.tensor.transpose(backs[b, half][:, c : c + P], middles[b, half][:, c : c + P], identity[:])
+
+        def finish(b, half):
+            cols = slice(half * R, (half + 1) * R)
+            result = keep.tile([P, R], F32, name="result%d_%d" % (b, half))
+            if VECTOR_COLS[b]:
+                nc.vector.tensor_tensor(result[:], backs[b, half][:], norm_rows[:, cols], SUBTRACT)
+            else:
+                nc.scalar.mul(result[:], backs[b, half][:], -1.0)
+            nc.sync.dma_start(out[b * P : (b + 1) * P, cols], result[:])
+
+        interleave(0, nc.vector.tensor_copy)
+        quantise(0)
         picked_words = late.tile([P, S], U32, name="picked_words", offset=0, align_bytes=64)
         pick_words(0)
         pick_words(1)
-        prepare(1)
-        steps = len(order)
-        for i in range(3):
-            multiply(i)
-        for i in range(2):
-            fill(i)
-        for i, (b, d) in enumerate(order):
-            if i + 3 < steps:
-                multiply(i + 3)
-            if i + 2 < steps:
-                fill(i + 2)
-            scalar_look_up(i)
-            if i >= 1 and order[i - 1][1] == BOOKS - 1:
-                turn_back(order[i - 1][0])
-            vector_look_up(i)
-            if i >= 2 and order[i - 2][1] == BOOKS - 1:
-                finish(order[i - 2][0])
-            if b == 0 and d in (1, 2):
-                prepare(d + 1)
-        turn_back(BLOCKS - 1)
-        finish(BLOCKS - 1)
+        interleave(1, nc.scalar.copy)
+        quantise(1)
+        multiply(0, 0)
+        multiply(0, 1)
+        multiply(1, 0)
+        multiply(0, 2)
+        fill(0, 0)
+        multiply(0, 3)
+        fill(0, 1)
+        multiply(1, 1)
+        fetch(0, 0, 256, 512)
+        chain(0, 0, 0, 128)
+        chain(0, 0, 128, 256)
+        fill(1, 0)
+        multiply(1, 2)
+        turn(0, 0, 256, 512)
+        fetch(0, 1, 256, 512)
+        chain(0, 1, 0, 128)
+        chain(0, 1, 128, 256)
+        fill(0, 2)
+        turn(0, 1, 256, 512)
+        interleave(2, nc.vector.tensor_copy, "sum0_0")
+        fill(0, 3)
+        fetch(0, 2, 256, 512)
+        chain(1, 0, 0, 512)
+        turn(0, 2, 256, 512)
+        fetch(0, 3, 256, 512)
+        quantise(2)
+        multiply(2, 0)
+        multiply(3, 0)
+        turn(0, 3, 256, 512)
+        fill(1, 1)
+        multiply(2, 1)
+        chain(0, 2, 0, 256)
+        fill(1, 2)
+        multiply(3, 1)
+        middle(0, 1)
+        fill(2, 0)
+        multiply(1, 3)
+        turn_back(0, 1)
+        chain(1, 1, 0, 512)
+        fill(3, 0)
+        multiply(2, 2)
+        fetch(2, 0, 0, 512)
+        chain(3, 0, 0, 512)
+        fill(2, 1)
+        multiply(2, 3)
+        turn(2, 0, 0, 512)
+        fill(3, 1)
+        multiply(3, 2)
+        fetch(2, 1, 0, 512)
+        chain(1, 2, 0, 512)
+        fill(1, 3)
+        multiply(3, 3)
+        turn(2, 1, 0, 512)
+        fill(2, 2)
+        chain(3, 1, 0, 512)
+        fetch(2, 2, 0, 512)
+        fill(2, 3)
+        turn(2, 2, 0, 512)
+        chain(1, 3, 0, 512)
+        fetch(2, 3, 0, 256)
+        turn(2, 3, 0, 256)
+        fill(3, 2)
+        finish(0, 1)
+        chain(0, 3, 0, 256)
+        fetch(2, 3, 256, 512)
+        turn(2, 3, 256, 512)
+        middle(2, 0)
+        turn_back(2, 0)
+        chain(3, 2, 0, 352)
+        fill(3, 3)
+        chain(3, 2, 352, 512)
+        middle(2, 1)
+        turn_back(2, 1)
+        chain(3, 3, 0, 352)
+        finish(2, 0)
+        chain(3, 3, 352, 512)
+        finish(2, 1)

@@ -23,11 +23,20 @@ PACK = 4
 LIST_ROWS = 16
 HALF = S // 2
 BLOCKS = V // P
-VECTOR_COLS = (256, 512, 0, 512)
+TURNED = 1
+CHAINS = {0: (0, 1, 2, 3), 2: (0, 1, 2, 3), 3: (0, 1, 2, 3)}
 SPARE = 16
 BLOCK_BYTES = PACK * P * 4
 VECTOR_SHARE = 520
-PRODUCT_BANKS = 4
+BANK_OF = {
+    (0, 0): 0, (0, 1): 1, (0, 2): 2, (1, 0): 3, (1, 1): 4,
+    (2, 0): 0, (3, 0): 1, (2, 1): 2, (3, 1): 3,
+    (0, 3): 0, (1, 2): 1, (1, 3): 2,
+    (2, 2): 0, (2, 3): 1, (3, 2): 2, (3, 3): 4,
+}
+TURNED_BANK = 3
+FOUND_AT = {(1, 3, 0): 12288, (2, 3, 256): 12288, (3, 3, 0): 13312, (3, 3, 256): 14336}
+MIDDLE_AT = 14336
 LAST_CUT = 352
 
 
@@ -52,8 +61,7 @@ def tile_picked_yadc_dist_p_kernel(
             nc.sync.dma_start(tile[:], code)
 
         def window_width(b, d):
-            longest = max(VECTOR_COLS[b], U - VECTOR_COLS[b])
-            return 2 * longest if d == 0 and VECTOR_COLS[b] else longest + SPARE
+            return 2 * U if b != TURNED and CHAINS[b][0] == d else U + SPARE
 
         windows = {
             (b, d): keep.tile([P, window_width(b, d)], F32, name="table%d_%d" % (b, d))
@@ -68,7 +76,7 @@ def tile_picked_yadc_dist_p_kernel(
         nc.vector.memset(cleared[:, VECTOR_SHARE - 7 : VECTOR_SHARE], 0)
         nc.gpsimd.memset(cleared[:, VECTOR_SHARE:], 0)
         nc.sync.dma_start(store_scales[32:96:4, :].bitcast(I32), x_scales[0].bitcast(I32))
-        nc.vector.tensor_copy(windows[0, 1][:, R:], zeros[:])
+        nc.vector.tensor_copy(windows[0, 1][:, U:], zeros[:])
         store_words = early.tile([P, T], U32, name="store_words", offset=0)
         word_rows = x_words[0].rearrange("p n t -> p (n t)").bitcast(I32)
         for lo in range(0, T, T // 2):
@@ -81,10 +89,11 @@ def tile_picked_yadc_dist_p_kernel(
 
         picked_scales = keep.tile([P, S], U8, name="picked_scales", align_bytes=64)
         nc.vector.memset(picked_scales[:].bitcast(I32), 0)
-        nc.vector.memset(windows[1, 0][:, R:], 0.0)
+        nc.vector.memset(windows[3, 0][:, R:], 0.0)
         for key, table in windows.items():
-            if key not in ((0, 1), (1, 0)):
-                nc.scalar.copy(table[:, R:], windows[1, 0][:, R : window_width(*key)])
+            if key != (3, 0):
+                end = U if key == (0, 1) else window_width(*key)
+                nc.scalar.copy(table[:, R:end], windows[3, 0][:, R:end])
         identity = keep.tile([P, P], F32, name="identity")
         make_identity(nc, identity[:])
 
@@ -101,7 +110,6 @@ def tile_picked_yadc_dist_p_kernel(
         raw23 = late.tile([P, PACK, 2 * P], F32, name="raw23", offset=4608 + BLOCK_BYTES)
         nc.sync.dma_start(raw23[:], h_rows[:, :, 2 * P :])
         raws = [raw0[:], raw1[:], raw23[:]]
-        widths = [P, P, 2 * P]
 
         h_codes = keep.tile([P, V], U32, name="h_codes", align_bytes=64)
         h_scales = keep.tile([P, V], U8, name="h_scales", align_bytes=64)
@@ -112,27 +120,29 @@ def tile_picked_yadc_dist_p_kernel(
                 picked_words[:, h * HALF : (h + 1) * HALF], store_words[:].indirect(picks[:, h * cols : (h + 1) * cols])
             )
 
-        grouped, banks, sums, turned, backs = {}, {}, {}, {}, {}
+        grouped, banks, sums = {}, {}, {}
 
         def interleave(b, copy, tag=None):
             if b == 0:
                 grouped[b] = late.tile([P, P, PACK], BF16, name="grouped0", offset=3584, align_bytes=64)
             else:
-                grouped[b] = keep.tile([P, widths[b], PACK], BF16, name="grouped%d" % b, tag=tag or "grouped%d" % b, align_bytes=64)
+                grouped[b] = keep.tile([P, b * P, PACK], BF16, name="grouped%d" % b, tag=tag or "grouped%d" % b, align_bytes=64)
+            target = grouped[b][:]
             copy(
-                grouped[b][:].rearrange("p (c i) j -> p c j i", i=4),
+                target.rearrange("p (c i) j -> p c j i", i=4),
                 raws[b].rearrange("p j (c i) -> p c j i", i=4),
             )
 
         def quantise(b):
+            width = max(b, 1) * P
             nc.vector.quantize_mx(
-                out=h_codes[:, b * P : b * P + widths[b]].bitcast(FP8X4),
-                scales=h_scales[:, b * P : b * P + widths[b]],
+                out=h_codes[:, b * P : b * P + width].bitcast(FP8X4),
+                scales=h_scales[:, b * P : b * P + width],
                 in_=grouped[b][:].rearrange("p t j -> p (t j)"),
             )
 
         def multiply(b, d):
-            banks[b, d] = psum.tile([P, R], F32, name="bank", tag="bank%d" % (len(banks) % PRODUCT_BANKS))
+            banks[b, d] = psum.tile([P, R], F32, name="bank", tag="bank%d" % BANK_OF[b, d])
             nc.tensor.matmul_mx(
                 out=banks[b, d][:],
                 lhsT=h_codes[:, b * P : (b + 1) * P].bitcast(FP8X4),
@@ -144,74 +154,70 @@ def tile_picked_yadc_dist_p_kernel(
             )
 
         def fill(b, d):
-            if VECTOR_COLS[b]:
-                nc.scalar.copy(windows[b, d][:, :R], banks[b, d][:])
-            else:
+            if b == TURNED:
                 nc.scalar.mul(windows[b, d][:, :R], banks[b, d][:], -1.0)
+            else:
+                nc.scalar.copy(windows[b, d][:, :R], banks[b, d][:])
 
         def entries(b, d, lo, hi):
             return windows[b, d][:].indirect(codes[d][:, lo // LIST_ROWS : hi // LIST_ROWS])
 
-        def chain(b, d, lo, hi):
-            if (b, d) not in sums:
-                sums[b, d] = keep.tile(
-                    [P, U], F32, name="sum%d_%d" % (b, d), tag="sum%d_%d" % (b, d), align_bytes=64
-                )
-            cols = slice(lo, hi)
-            if d == 0:
-                nc.vector.tensor_tensor(sums[b, d][:, cols], entries(b, d, lo, hi), norm_rows[:, cols], SUBTRACT)
-            else:
-                nc.vector.tensor_tensor(sums[b, d][:, cols], entries(b, d, lo, hi), sums[b, d - 1][:, cols], ADD)
-            if d == BOOKS - 1:
-                nc.sync.dma_start(out[b * P : (b + 1) * P, cols], sums[b, d][:, cols])
-
         found = {}
 
         def fetch(b, d, lo, hi):
-            found[b, d, lo] = keep.tile([P, hi - lo], F32, name="found%d_%d_%d" % (b, d, lo))
+            name = "found%d_%d_%d" % (b, d, lo)
+            if (b, d, lo) in FOUND_AT:
+                found[b, d, lo] = late.tile([P, hi - lo], F32, name=name, offset=FOUND_AT[b, d, lo])
+            else:
+                found[b, d, lo] = keep.tile([P, hi - lo], F32, name=name)
             nc.scalar.activation(found[b, d, lo][:], entries(b, d, lo, hi), COPY)
 
-        def add_turned(b, half, source, first, last):
-            if first:
-                turned[b, half] = psum.tile([P, R], F32, name="turned", tag="turned%d" % (len(turned) % 2))
-            for c in range(0, R, P):
+        def chain(b, d, lo, hi, fetched=False):
+            if (b, d) == (0, 1):
+                sums[b, d] = late.tile([P, U], F32, name="sum0_1", offset=4608 + BLOCK_BYTES)
+            elif (b, d) not in sums:
+                sums[b, d] = keep.tile([P, U], F32, name="sum%d_%d" % (b, d), tag="sum%d_%d" % (b, d), align_bytes=64)
+            cols = slice(lo, hi)
+            place = CHAINS[b].index(d)
+            source = found[b, d, lo][:] if fetched else entries(b, d, lo, hi)
+            if place == 0:
+                nc.vector.tensor_tensor(sums[b, d][:, cols], source, norm_rows[:, cols], SUBTRACT)
+            else:
+                nc.vector.tensor_tensor(sums[b, d][:, cols], source, sums[b, CHAINS[b][place - 1]][:, cols], ADD)
+            if place == BOOKS - 1:
+                nc.sync.dma_start(out[b * P : (b + 1) * P, cols], sums[b, d][:, cols])
+
+        turned = []
+
+        def add_turned(source, first, last):
+            for c in range(0, U, P):
                 nc.tensor.matmul(
-                    turned[b, half][:, c : c + P],
+                    turned[0][:, c : c + P],
                     source[:, c : c + P],
                     identity[:],
                     is_transpose=True,
                     start=(first and c == 0),
-                    stop=(last and c == R - P),
+                    stop=(last and c == U - P),
                 )
 
-        def turn(b, d, lo, hi):
-            for at in range(lo, hi, R):
-                half = at // R
-                if d == 0 and not VECTOR_COLS[b]:
-                    add_turned(b, half, norm_rows[:, at : at + R], True, False)
-                add_turned(
-                    b, half, found[b, d, lo][:, at - lo : at - lo + R], d == 0 and VECTOR_COLS[b] > 0, d == BOOKS - 1
-                )
+        def turn(d):
+            if d == 0:
+                turned.append(psum.tile([P, U], F32, name="turned", tag="bank%d" % TURNED_BANK))
+                add_turned(norm_rows, True, False)
+            add_turned(found[TURNED, d, 0], False, d == BOOKS - 1)
 
-        middles = {}
+        middle = late.tile([P, U], F32, name="middle", offset=MIDDLE_AT)
+        back = psum.tile([P, U], F32, name="back")
+        result = keep.tile([P, U], F32, name="result")
 
-        def middle(b, half):
-            middles[b, half] = keep.tile([P, R], F32, name="middle%d_%d" % (b, half))
-            nc.scalar.copy(middles[b, half][:], turned[b, half][:])
+        def turn_back():
+            nc.scalar.copy(middle[:], turned[0][:])
+            for c in range(0, U, P):
+                nc.tensor.transpose(back[:, c : c + P], middle[:, c : c + P], identity[:])
 
-        def turn_back(b, half):
-            backs[b, half] = psum.tile([P, R], F32, name="back", tag="back%d" % (len(backs) % 2))
-            for c in range(0, R, P):
-                nc.tensor.transpose(backs[b, half][:, c : c + P], middles[b, half][:, c : c + P], identity[:])
-
-        def finish(b, half):
-            cols = slice(half * R, (half + 1) * R)
-            result = keep.tile([P, R], F32, name="result%d_%d" % (b, half))
-            if VECTOR_COLS[b]:
-                nc.vector.tensor_tensor(result[:], backs[b, half][:], norm_rows[:, cols], SUBTRACT)
-            else:
-                nc.scalar.mul(result[:], backs[b, half][:], -1.0)
-            nc.sync.dma_start(out[b * P : (b + 1) * P, cols], result[:])
+        def finish():
+            nc.scalar.mul(result[:], back[:], -1.0)
+            nc.sync.dma_start(out[TURNED * P : (TURNED + 1) * P, :], result[:])
 
         interleave(0, nc.vector.tensor_copy)
         quantise(0)
@@ -222,78 +228,63 @@ def tile_picked_yadc_dist_p_kernel(
         quantise(1)
         multiply(0, 0)
         multiply(0, 1)
-        multiply(1, 0)
         multiply(0, 2)
-        fill(0, 0)
-        multiply(0, 3)
-        fill(0, 1)
+        multiply(1, 0)
         multiply(1, 1)
-        fetch(0, 0, 256, 512)
-        chain(0, 0, 0, 128)
-        chain(0, 0, 128, 256)
-        fill(1, 0)
-        multiply(1, 2)
-        turn(0, 0, 256, 512)
-        fetch(0, 1, 256, 512)
-        chain(0, 1, 0, 128)
-        chain(0, 1, 128, 256)
+        fill(0, 0)
+        fill(0, 1)
+        chain(0, 0, 0, 512)
         fill(0, 2)
-        turn(0, 1, 256, 512)
-        interleave(2, nc.vector.tensor_copy, "sum0_0")
-        fill(0, 3)
-        fetch(0, 2, 256, 512)
-        chain(1, 0, 0, 512)
-        turn(0, 2, 256, 512)
-        fetch(0, 3, 256, 512)
+        fill(1, 0)
+        fetch(1, 0, 0, 512)
+        interleave(2, nc.vector.tensor_copy, "sum0_2")
+        chain(0, 1, 0, 512)
+        fill(1, 1)
+        fetch(1, 1, 0, 512)
         quantise(2)
         multiply(2, 0)
         multiply(3, 0)
-        turn(0, 3, 256, 512)
-        fill(1, 1)
         multiply(2, 1)
-        chain(0, 2, 0, 256)
-        fill(1, 2)
         multiply(3, 1)
-        middle(0, 1)
+        chain(0, 2, 0, 512)
         fill(2, 0)
-        multiply(1, 3)
-        turn_back(0, 1)
-        chain(1, 1, 0, 512)
+        multiply(0, 3)
         fill(3, 0)
-        multiply(2, 2)
-        fetch(2, 0, 0, 512)
-        chain(3, 0, 0, 512)
+        multiply(1, 2)
         fill(2, 1)
-        multiply(2, 3)
-        turn(2, 0, 0, 512)
+        multiply(1, 3)
         fill(3, 1)
-        multiply(3, 2)
-        fetch(2, 1, 0, 512)
-        chain(1, 2, 0, 512)
-        fill(1, 3)
+        fill(0, 3)
+        multiply(2, 2)
+        fill(1, 2)
+        multiply(2, 3)
         multiply(3, 3)
-        turn(2, 1, 0, 512)
+        chain(2, 0, 0, 512)
+        turn(0)
+        turn(1)
+        fetch(1, 2, 0, 512)
+        chain(0, 3, 0, 512)
+        fill(1, 3)
+        multiply(3, 2)
+        turn(2)
+        fetch(1, 3, 0, 512)
+        chain(2, 1, 0, 512)
+        turn(3)
+        chain(3, 0, 0, 512)
         fill(2, 2)
-        chain(3, 1, 0, 512)
-        fetch(2, 2, 0, 512)
         fill(2, 3)
-        turn(2, 2, 0, 512)
-        chain(1, 3, 0, 512)
-        fetch(2, 3, 0, 256)
-        turn(2, 3, 0, 256)
         fill(3, 2)
-        finish(0, 1)
-        chain(0, 3, 0, 256)
-        fetch(2, 3, 256, 512)
-        turn(2, 3, 256, 512)
-        middle(2, 0)
-        turn_back(2, 0)
-        chain(3, 2, 0, 352)
         fill(3, 3)
-        chain(3, 2, 352, 512)
-        middle(2, 1)
-        turn_back(2, 1)
-        chain(3, 3, 0, 352)
-        finish(2, 0)
-        chain(3, 3, 352, 512)
-        finish(2, 1)
+        chain(2, 2, 0, 512)
+        turn_back()
+        fetch(2, 3, 256, 512)
+        chain(3, 1, 0, 512)
+        fetch(3, 3, 0, 256)
+        chain(2, 3, 0, 256)
+        finish()
+        chain(2, 3, 256, 512, True)
+        fetch(3, 3, 256, 512)
+        chain(3, 2, 0, 256)
+        chain(3, 2, 256, 512)
+        chain(3, 3, 0, 256, True)
+        chain(3, 3, 256, 512, True)

@@ -24,19 +24,19 @@ LIST_ROWS = 16
 HALF = S // 2
 BLOCKS = V // P
 TURNED = 1
-CHAINS = {0: (0, 1, 2, 3), 2: (0, 1, 2, 3), 3: (0, 1, 2, 3)}
+CHAINS = {0: (1, 2, 0, 3), 2: (0, 1, 2, 3), 3: (0, 1, 2, 3)}
 SPARE = 16
 BLOCK_BYTES = PACK * P * 4
 VECTOR_SHARE = 520
 BANK_OF = {
-    (0, 0): 0, (0, 1): 1, (0, 2): 2, (1, 0): 3, (1, 1): 4,
+    (0, 1): 0, (0, 0): 1, (0, 2): 2, (1, 0): 3, (1, 1): 4, (0, 3): 5,
     (2, 0): 0, (3, 0): 1, (2, 1): 2, (3, 1): 3,
-    (0, 3): 0, (1, 2): 1, (1, 3): 2,
-    (2, 2): 0, (2, 3): 1, (3, 2): 2, (3, 3): 4,
+    (1, 2): 0, (1, 3): 1,
+    (2, 2): 2, (2, 3): 0, (3, 2): 1, (3, 3): 4,
 }
 TURNED_BANK = 3
-FOUND_AT = {(1, 3, 0): 12288, (2, 3, 256): 12288, (3, 3, 0): 13312, (3, 3, 256): 14336}
-MIDDLE_AT = 14336
+FOUND_AT = {(1, 3, 0): 12288, (2, 3, 0): 13312, (3, 3, 256): 12288}
+MIDDLE_AT = 18432
 LAST_CUT = 352
 
 
@@ -76,7 +76,7 @@ def tile_picked_yadc_dist_p_kernel(
         nc.vector.memset(cleared[:, VECTOR_SHARE - 7 : VECTOR_SHARE], 0)
         nc.gpsimd.memset(cleared[:, VECTOR_SHARE:], 0)
         nc.sync.dma_start(store_scales[32:96:4, :].bitcast(I32), x_scales[0].bitcast(I32))
-        nc.vector.tensor_copy(windows[0, 1][:, U:], zeros[:])
+        nc.vector.tensor_copy(windows[0, 0][:, U:], zeros[:])
         store_words = early.tile([P, T], U32, name="store_words", offset=0)
         word_rows = x_words[0].rearrange("p n t -> p (n t)").bitcast(I32)
         for lo in range(0, T, T // 2):
@@ -92,7 +92,7 @@ def tile_picked_yadc_dist_p_kernel(
         nc.vector.memset(windows[3, 0][:, R:], 0.0)
         for key, table in windows.items():
             if key != (3, 0):
-                end = U if key == (0, 1) else window_width(*key)
+                end = U if key == (0, 0) else window_width(*key)
                 nc.scalar.copy(table[:, R:end], windows[3, 0][:, R:end])
         identity = keep.tile([P, P], F32, name="identity")
         make_identity(nc, identity[:])
@@ -129,8 +129,8 @@ def tile_picked_yadc_dist_p_kernel(
                 grouped[b] = keep.tile([P, b * P, PACK], BF16, name="grouped%d" % b, tag=tag or "grouped%d" % b, align_bytes=64)
             target = grouped[b][:]
             copy(
-                target.rearrange("p (c i) j -> p c j i", i=4),
-                raws[b].rearrange("p j (c i) -> p c j i", i=4),
+                target,
+                raws[b].rearrange("p j t -> p t j"),
             )
 
         def quantise(b):
@@ -165,6 +165,11 @@ def tile_picked_yadc_dist_p_kernel(
         found = {}
 
         def fetch(b, d, lo, hi):
+            if (b, d) == (0, 0):
+                if lo == 0:
+                    found[b, d, lo] = keep.tile([P, U], F32, name="found0_0")
+                nc.scalar.activation(found[b, d, 0][:, lo:hi], entries(b, d, lo, hi), COPY)
+                return
             name = "found%d_%d_%d" % (b, d, lo)
             if (b, d, lo) in FOUND_AT:
                 found[b, d, lo] = late.tile([P, hi - lo], F32, name=name, offset=FOUND_AT[b, d, lo])
@@ -173,8 +178,10 @@ def tile_picked_yadc_dist_p_kernel(
             nc.scalar.activation(found[b, d, lo][:], entries(b, d, lo, hi), COPY)
 
         def chain(b, d, lo, hi, fetched=False):
-            if (b, d) == (0, 1):
-                sums[b, d] = late.tile([P, U], F32, name="sum0_1", offset=4608 + BLOCK_BYTES)
+            if (b, d, lo) == (0, 0, 0):
+                sums[b, d] = late.tile([P, U], F32, name="sum0_0", offset=4608 + BLOCK_BYTES)
+            elif (b, d, lo) == (3, 3, 0):
+                sums[b, d] = late.tile([P, U], F32, name="sum3_3", offset=FOUND_AT[2, 3, 0] + 1024)
             elif (b, d) not in sums:
                 sums[b, d] = keep.tile([P, U], F32, name="sum%d_%d" % (b, d), tag="sum%d_%d" % (b, d), align_bytes=64)
             cols = slice(lo, hi)
@@ -231,60 +238,61 @@ def tile_picked_yadc_dist_p_kernel(
         multiply(0, 2)
         multiply(1, 0)
         multiply(1, 1)
+        multiply(0, 3)
         fill(0, 0)
         fill(0, 1)
-        chain(0, 0, 0, 512)
+        fetch(0, 0, 0, 256)
+        chain(0, 1, 0, 256)
+        chain(0, 1, 256, 512)
         fill(0, 2)
+        fetch(0, 0, 256, 512)
         fill(1, 0)
-        fetch(1, 0, 0, 512)
-        interleave(2, nc.vector.tensor_copy, "sum0_2")
-        chain(0, 1, 0, 512)
         fill(1, 1)
+        chain(0, 2, 0, 256)
+        chain(0, 2, 256, 512)
+        fetch(1, 0, 0, 512)
+        fill(0, 3)
+        interleave(2, nc.vector.tensor_copy, "sum0_3")
         fetch(1, 1, 0, 512)
+        chain(0, 0, 0, 512, True)
         quantise(2)
         multiply(2, 0)
         multiply(3, 0)
         multiply(2, 1)
         multiply(3, 1)
-        chain(0, 2, 0, 512)
+        chain(0, 3, 0, 512)
         fill(2, 0)
-        multiply(0, 3)
-        fill(3, 0)
         multiply(1, 2)
-        fill(2, 1)
+        fill(3, 0)
         multiply(1, 3)
-        fill(3, 1)
-        fill(0, 3)
+        fill(2, 1)
         multiply(2, 2)
+        fill(3, 1)
         fill(1, 2)
         multiply(2, 3)
         multiply(3, 3)
+        fill(1, 3)
+        multiply(3, 2)
         chain(2, 0, 0, 512)
         turn(0)
         turn(1)
         fetch(1, 2, 0, 512)
-        chain(0, 3, 0, 512)
-        fill(1, 3)
-        multiply(3, 2)
+        chain(3, 0, 0, 512)
         turn(2)
         fetch(1, 3, 0, 512)
         chain(2, 1, 0, 512)
         turn(3)
-        chain(3, 0, 0, 512)
         fill(2, 2)
         fill(2, 3)
         fill(3, 2)
         fill(3, 3)
-        chain(2, 2, 0, 512)
-        turn_back()
-        fetch(2, 3, 256, 512)
         chain(3, 1, 0, 512)
-        fetch(3, 3, 0, 256)
-        chain(2, 3, 0, 256)
-        finish()
-        chain(2, 3, 256, 512, True)
+        turn_back()
+        chain(2, 2, 0, 512)
+        fetch(2, 3, 0, 512)
+        chain(3, 2, 0, 512)
         fetch(3, 3, 256, 512)
-        chain(3, 2, 0, 256)
-        chain(3, 2, 256, 512)
-        chain(3, 3, 0, 256, True)
+        chain(2, 3, 0, 512, True)
+        finish()
+        chain(3, 3, 0, 256)
         chain(3, 3, 256, 512, True)

@@ -21,23 +21,31 @@ COPY = mybir.ActivationFunctionType.Copy
 P = 128
 PACK = 4
 LIST_ROWS = 16
-HALF = S // 2
-BLOCKS = V // P
-TURNED = 1
-CHAINS = {0: (1, 2, 0, 3), 2: (0, 1, 2, 3), 3: (0, 1, 2, 3)}
+BATCHES = V // P
+HALF_PICKS = S // 2
+HALF_OUT = U // 2
+SCALAR_BATCH = 1
+SHARED_COLS = U - P
+SHARED_HALF = SHARED_COLS // 2
 SPARE = 16
-BLOCK_BYTES = PACK * P * 4
 VECTOR_SHARE = 520
+ODD_REST = 7
+
 BANK_OF = {
-    (0, 1): 0, (0, 0): 1, (0, 2): 2, (1, 0): 3, (1, 1): 4, (0, 3): 5,
-    (2, 0): 0, (3, 0): 1, (2, 1): 2, (3, 1): 3,
-    (1, 2): 0, (1, 3): 1,
-    (2, 2): 2, (2, 3): 0, (3, 2): 1, (3, 3): 4,
+    (0, 0): 0, (0, 1): 1, (0, 2): 2, (1, 0): 3, (0, 3): 4,
+    (2, 0): 0, (3, 0): 1, (2, 1): 2, (3, 1): 3, (2, 2): 4,
+    (1, 1): 0, (1, 2): 1, (1, 3): 2,
+    (3, 2): 6, (2, 3): 7, (3, 3): 0,
 }
-TURNED_BANK = 3
-FOUND_AT = {(1, 3, 0): 12288, (2, 3, 0): 13312, (3, 3, 256): 12288}
-MIDDLE_AT = 18432
-LAST_CUT = 352
+GROUP_BANK = {(0, SHARED_COLS): 5, (SCALAR_BATCH, 0): 3, (SCALAR_BATCH, HALF_OUT): 4}
+
+FIRST_WORDS_AT = 2048
+GROUPED0_AT = 3584
+SCALE_TABLE_AT = 4096
+NORM_AT = 4608
+RAW23_AT = NORM_AT + 4 * U
+GROUPED23_AT = 12288
+LAST_FETCH_AT = 16384
 
 
 def tile_picked_yadc_dist_p_kernel(
@@ -60,23 +68,25 @@ def tile_picked_yadc_dist_p_kernel(
         for tile, code in zip(codes[:2], (code1, code2)):
             nc.sync.dma_start(tile[:], code)
 
-        def window_width(b, d):
-            return 2 * U if b != TURNED and CHAINS[b][0] == d else U + SPARE
+        def table_width(b, d):
+            longest = SHARED_COLS if b == 0 else U
+            return 2 * longest if b != SCALAR_BATCH and d == 0 else longest + SPARE
 
-        windows = {
-            (b, d): keep.tile([P, window_width(b, d)], F32, name="table%d_%d" % (b, d))
-            for b in range(BLOCKS)
+        tables = {
+            (b, d): keep.tile([P, table_width(b, d)], F32, name="table%d_%d" % (b, d))
+            for b in range(BATCHES)
             for d in range(BOOKS)
         }
-        zeros = early.tile([P, SPARE], F32, name="zeros", offset=4 * T - 32)
+
+        zeros = early.tile([P, SPARE - 1], F32, name="zeros", offset=4 * T - 32)
         nc.vector.memset(zeros[:], 0.0)
-        store_scales = late.tile([P, T], U8, name="store_scales", offset=4096)
+        store_scales = late.tile([P, T], U8, name="store_scales", offset=SCALE_TABLE_AT)
         cleared = store_scales[:].bitcast(U32)
-        nc.vector.memset(cleared[:, : VECTOR_SHARE - 7], 0)
-        nc.vector.memset(cleared[:, VECTOR_SHARE - 7 : VECTOR_SHARE], 0)
+        nc.vector.memset(cleared[:, : VECTOR_SHARE - ODD_REST], 0)
+        nc.vector.memset(cleared[:, VECTOR_SHARE - ODD_REST : VECTOR_SHARE], 0)
         nc.gpsimd.memset(cleared[:, VECTOR_SHARE:], 0)
         nc.sync.dma_start(store_scales[32:96:4, :].bitcast(I32), x_scales[0].bitcast(I32))
-        nc.vector.tensor_copy(windows[0, 0][:, U:], zeros[:])
+        nc.vector.tensor_copy(tables[0, 1][:, SHARED_COLS + 1 :], zeros[:])
         store_words = early.tile([P, T], U32, name="store_words", offset=0)
         word_rows = x_words[0].rearrange("p n t -> p (n t)").bitcast(I32)
         for lo in range(0, T, T // 2):
@@ -89,11 +99,11 @@ def tile_picked_yadc_dist_p_kernel(
 
         picked_scales = keep.tile([P, S], U8, name="picked_scales", align_bytes=64)
         nc.vector.memset(picked_scales[:].bitcast(I32), 0)
-        nc.vector.memset(windows[3, 0][:, R:], 0.0)
-        for key, table in windows.items():
+        nc.vector.memset(tables[3, 0][:, R:], 0.0)
+        for key, table in tables.items():
             if key != (3, 0):
-                end = U if key == (0, 0) else window_width(*key)
-                nc.scalar.copy(table[:, R:end], windows[3, 0][:, R:end])
+                end = SHARED_COLS + 1 if key == (0, 1) else table_width(*key)
+                nc.scalar.copy(table[:, R:end], tables[3, 0][:, R:end])
         identity = keep.tile([P, P], F32, name="identity")
         make_identity(nc, identity[:])
 
@@ -105,39 +115,38 @@ def tile_picked_yadc_dist_p_kernel(
                 spread_scales[32 + 4 * r : 96 : 16, :].bitcast(I32),
             )
 
-        norm_rows = late.tile([P, U], F32, name="norm_rows", offset=4608)
+        norm_rows = late.tile([P, U], F32, name="norm_rows", offset=NORM_AT)
         nc.sync.dma_start(norm_rows[:], norm)
-        raw23 = late.tile([P, PACK, 2 * P], F32, name="raw23", offset=4608 + BLOCK_BYTES)
+        raw23 = late.tile([P, PACK, 2 * P], F32, name="raw23", offset=RAW23_AT)
         nc.sync.dma_start(raw23[:], h_rows[:, :, 2 * P :])
-        raws = [raw0[:], raw1[:], raw23[:]]
+        raws = [raw0, raw1, raw23]
 
         h_codes = keep.tile([P, V], U32, name="h_codes", align_bytes=64)
         h_scales = keep.tile([P, V], U8, name="h_scales", align_bytes=64)
 
+        grouped, banks, sums, found, groups, backs = {}, {}, {}, {}, {}, {}
+
         def pick_words(h):
-            cols = HALF // LIST_ROWS
-            nc.vector.tensor_copy(
-                picked_words[:, h * HALF : (h + 1) * HALF], store_words[:].indirect(picks[:, h * cols : (h + 1) * cols])
-            )
+            cols = HALF_PICKS // LIST_ROWS
+            nc.vector.tensor_copy(picked_words[h][:], store_words[:].indirect(picks[:, h * cols : (h + 1) * cols]))
 
-        grouped, banks, sums = {}, {}, {}
-
-        def interleave(b, copy, tag=None):
+        def interleave(b, copy):
             if b == 0:
-                grouped[b] = late.tile([P, P, PACK], BF16, name="grouped0", offset=3584, align_bytes=64)
+                grouped[b] = late.tile([P, P, PACK], BF16, name="grouped0", offset=GROUPED0_AT, align_bytes=64)
+            elif b == 1:
+                grouped[b] = keep.tile([P, P, PACK], BF16, name="grouped1", align_bytes=64)
             else:
-                grouped[b] = keep.tile([P, b * P, PACK], BF16, name="grouped%d" % b, tag=tag or "grouped%d" % b, align_bytes=64)
-            target = grouped[b][:]
+                grouped[b] = late.tile([P, 2 * P, PACK], BF16, name="grouped23", offset=GROUPED23_AT, align_bytes=64)
             copy(
-                target,
-                raws[b].rearrange("p j t -> p t j"),
+                grouped[b][:].rearrange("p (c i) j -> p c j i", i=4),
+                raws[b][:].rearrange("p j (c i) -> p c j i", i=4),
             )
 
         def quantise(b):
-            width = max(b, 1) * P
+            cols = slice(b * P, b * P + grouped[b].shape[1])
             nc.vector.quantize_mx(
-                out=h_codes[:, b * P : b * P + width].bitcast(FP8X4),
-                scales=h_scales[:, b * P : b * P + width],
+                out=h_codes[:, cols].bitcast(FP8X4),
+                scales=h_scales[:, cols],
                 in_=grouped[b][:].rearrange("p t j -> p (t j)"),
             )
 
@@ -147,152 +156,173 @@ def tile_picked_yadc_dist_p_kernel(
                 out=banks[b, d][:],
                 lhsT=h_codes[:, b * P : (b + 1) * P].bitcast(FP8X4),
                 lhsT_scale=h_scales[:, b * P : (b + 1) * P],
-                rhs=picked_words[:, d * R : (d + 1) * R].bitcast(FP8X4),
+                rhs=picked_words[d // 2][:, d % 2 * R : (d % 2 + 1) * R].bitcast(FP8X4),
                 rhs_scale=picked_scales[:, d * R : (d + 1) * R],
                 start=True,
                 stop=True,
             )
 
         def fill(b, d):
-            if b == TURNED:
-                nc.scalar.mul(windows[b, d][:, :R], banks[b, d][:], -1.0)
+            if b == SCALAR_BATCH:
+                nc.scalar.mul(tables[b, d][:, :R], banks[b, d][:], -1.0)
             else:
-                nc.scalar.copy(windows[b, d][:, :R], banks[b, d][:])
+                nc.scalar.copy(tables[b, d][:, :R], banks[b, d][:])
 
         def entries(b, d, lo, hi):
-            return windows[b, d][:].indirect(codes[d][:, lo // LIST_ROWS : hi // LIST_ROWS])
-
-        found = {}
+            return tables[b, d][:].indirect(codes[d][:, lo // LIST_ROWS : hi // LIST_ROWS])
 
         def fetch(b, d, lo, hi):
-            if (b, d) == (0, 0):
-                if lo == 0:
-                    found[b, d, lo] = keep.tile([P, U], F32, name="found0_0")
-                nc.scalar.activation(found[b, d, 0][:, lo:hi], entries(b, d, lo, hi), COPY)
-                return
             name = "found%d_%d_%d" % (b, d, lo)
-            if (b, d, lo) in FOUND_AT:
-                found[b, d, lo] = late.tile([P, hi - lo], F32, name=name, offset=FOUND_AT[b, d, lo])
+            if d == BOOKS - 1 and lo == HALF_OUT:
+                found[b, d, lo] = late.tile([P, hi - lo], F32, name=name, offset=LAST_FETCH_AT)
             else:
                 found[b, d, lo] = keep.tile([P, hi - lo], F32, name=name)
-            nc.scalar.activation(found[b, d, lo][:], entries(b, d, lo, hi), COPY)
-
-        def chain(b, d, lo, hi, fetched=False):
-            if (b, d, lo) == (0, 0, 0):
-                sums[b, d] = late.tile([P, U], F32, name="sum0_0", offset=4608 + BLOCK_BYTES)
-            elif (b, d, lo) == (3, 3, 0):
-                sums[b, d] = late.tile([P, U], F32, name="sum3_3", offset=FOUND_AT[2, 3, 0] + 1024)
-            elif (b, d) not in sums:
-                sums[b, d] = keep.tile([P, U], F32, name="sum%d_%d" % (b, d), tag="sum%d_%d" % (b, d), align_bytes=64)
-            cols = slice(lo, hi)
-            place = CHAINS[b].index(d)
-            source = found[b, d, lo][:] if fetched else entries(b, d, lo, hi)
-            if place == 0:
-                nc.vector.tensor_tensor(sums[b, d][:, cols], source, norm_rows[:, cols], SUBTRACT)
+            if b == 0:
+                nc.scalar.activation(found[b, d, lo][:], entries(b, d, lo, hi), COPY, scale=-1.0)
             else:
-                nc.vector.tensor_tensor(sums[b, d][:, cols], source, sums[b, CHAINS[b][place - 1]][:, cols], ADD)
-            if place == BOOKS - 1:
+                nc.scalar.activation(found[b, d, lo][:], entries(b, d, lo, hi), COPY)
+
+        def sum_tile(b, d):
+            if (b, d) == (0, 1):
+                return late.tile([P, SHARED_COLS], F32, name="sum0_1", offset=RAW23_AT)
+            if (b, d) == (0, 2):
+                return late.tile([P, SHARED_COLS], F32, name="sum0_2", offset=GROUPED23_AT)
+            return keep.tile([P, U], F32, name="sum%d_%d" % (b, d))
+
+        def step(b, d, lo, hi, values):
+            cols = slice(lo, hi)
+            if (b, d) not in sums:
+                sums[b, d] = sum_tile(b, d)
+            if d == 0:
+                nc.vector.tensor_tensor(sums[b, d][:, cols], values, norm_rows[:, cols], SUBTRACT)
+            else:
+                nc.vector.tensor_tensor(sums[b, d][:, cols], values, sums[b, d - 1][:, cols], ADD)
+            if d == BOOKS - 1:
                 nc.sync.dma_start(out[b * P : (b + 1) * P, cols], sums[b, d][:, cols])
 
-        turned = []
+        def look_up(b, d, lo=0, hi=U):
+            step(b, d, lo, hi, entries(b, d, lo, hi))
 
-        def add_turned(source, first, last):
-            for c in range(0, U, P):
+        def look_up_in_halves(d):
+            for lo in (0, SHARED_HALF):
+                look_up(0, d, lo, lo + SHARED_HALF)
+
+        def add_to_group(b, at, width, source, first, last):
+            if first:
+                groups[b, at] = psum.tile([P, width], F32, name="group", tag="bank%d" % GROUP_BANK[b, at])
+            for c in range(0, width, P):
                 nc.tensor.matmul(
-                    turned[0][:, c : c + P],
+                    groups[b, at][:, c : c + P],
                     source[:, c : c + P],
                     identity[:],
                     is_transpose=True,
                     start=(first and c == 0),
-                    stop=(last and c == U - P),
+                    stop=(last and c == width - P),
                 )
 
-        def turn(d):
-            if d == 0:
-                turned.append(psum.tile([P, U], F32, name="turned", tag="bank%d" % TURNED_BANK))
-                add_turned(norm_rows, True, False)
-            add_turned(found[TURNED, d, 0], False, d == BOOKS - 1)
+        def turn(b, d, lo, hi):
+            width = min(hi - lo, HALF_OUT)
+            for at in range(lo, hi, width):
+                norm_first = d == 0 and b == SCALAR_BATCH
+                if norm_first:
+                    add_to_group(b, at, width, norm_rows[:, at : at + width], True, False)
+                source = found[b, d, lo][:, at - lo : at - lo + width]
+                add_to_group(b, at, width, source, d == 0 and not norm_first, d == BOOKS - 1)
+                if d == 1 and b == 0:
+                    add_to_group(b, at, width, norm_rows[:, at : at + width], False, False)
 
-        middle = late.tile([P, U], F32, name="middle", offset=MIDDLE_AT)
-        back = psum.tile([P, U], F32, name="back")
-        result = keep.tile([P, U], F32, name="result")
+        def turn_back(b, lo, hi):
+            name = "middle%d_%d" % (b, lo)
+            if b == 0:
+                middle = late.tile([P, hi - lo], F32, name=name, offset=FIRST_WORDS_AT)
+            else:
+                middle = keep.tile([P, hi - lo], F32, name=name)
+            nc.scalar.copy(middle[:], groups[b, lo][:])
+            backs[b, lo] = psum.tile([P, hi - lo], F32, name="back", tag="bank%d" % GROUP_BANK[b, lo])
+            for c in range(0, hi - lo, P):
+                nc.tensor.transpose(backs[b, lo][:, c : c + P], middle[:, c : c + P], identity[:])
 
-        def turn_back():
-            nc.scalar.copy(middle[:], turned[0][:])
-            for c in range(0, U, P):
-                nc.tensor.transpose(back[:, c : c + P], middle[:, c : c + P], identity[:])
-
-        def finish():
-            nc.scalar.mul(result[:], back[:], -1.0)
-            nc.sync.dma_start(out[TURNED * P : (TURNED + 1) * P, :], result[:])
+        def finish(b, lo, hi):
+            result = keep.tile([P, hi - lo], F32, name="result%d_%d" % (b, lo))
+            nc.scalar.mul(result[:], backs[b, lo][:], -1.0)
+            queue = nc.sync if b == 0 else nc.scalar
+            queue.dma_start(out[b * P : (b + 1) * P, lo:hi], result[:])
 
         interleave(0, nc.vector.tensor_copy)
         quantise(0)
-        picked_words = late.tile([P, S], U32, name="picked_words", offset=0, align_bytes=64)
+        picked_words = [
+            late.tile([P, HALF_PICKS], U32, name="picked_words0", offset=FIRST_WORDS_AT, align_bytes=64),
+            keep.tile([P, HALF_PICKS], U32, name="picked_words1", align_bytes=64),
+        ]
         pick_words(0)
         pick_words(1)
         interleave(1, nc.scalar.copy)
         quantise(1)
-        multiply(0, 0)
-        multiply(0, 1)
-        multiply(0, 2)
+
+        for d in range(BOOKS):
+            multiply(0, d)
         multiply(1, 0)
-        multiply(1, 1)
-        multiply(0, 3)
         fill(0, 0)
         fill(0, 1)
-        fetch(0, 0, 0, 256)
-        chain(0, 1, 0, 256)
-        chain(0, 1, 256, 512)
+        fetch(0, 0, SHARED_COLS, U)
+        look_up(0, 0, 0, SHARED_COLS)
         fill(0, 2)
-        fetch(0, 0, 256, 512)
-        fill(1, 0)
-        fill(1, 1)
-        chain(0, 2, 0, 256)
-        chain(0, 2, 256, 512)
-        fetch(1, 0, 0, 512)
         fill(0, 3)
-        interleave(2, nc.vector.tensor_copy, "sum0_3")
-        fetch(1, 1, 0, 512)
-        chain(0, 0, 0, 512, True)
+        interleave(2, nc.vector.tensor_copy)
+        fetch(0, 1, SHARED_COLS, U)
+        fetch(0, 2, SHARED_COLS, U)
+        fill(1, 0)
+        turn(0, 0, SHARED_COLS, U)
+        turn(0, 1, SHARED_COLS, U)
+        look_up(0, 1, 0, SHARED_HALF)
+        fetch(0, 3, SHARED_COLS, U)
         quantise(2)
-        multiply(2, 0)
-        multiply(3, 0)
-        multiply(2, 1)
-        multiply(3, 1)
-        chain(0, 3, 0, 512)
-        fill(2, 0)
-        multiply(1, 2)
-        fill(3, 0)
-        multiply(1, 3)
-        fill(2, 1)
-        multiply(2, 2)
-        fill(3, 1)
+        look_up(0, 1, SHARED_HALF, SHARED_COLS)
+        fetch(1, 0, 0, U)
+        turn(0, 2, SHARED_COLS, U)
+        turn(0, 3, SHARED_COLS, U)
+
+        run = [(2, 0), (3, 0), (2, 1), (3, 1), (2, 2)]
+        for b, d in run:
+            multiply(b, d)
+        look_up_in_halves(2)
+        for i, (b, d) in enumerate(run):
+            fill(b, d)
+            if i + 1 < BOOKS:
+                multiply(1, i + 1)
+        look_up_in_halves(3)
+        fill(1, 1)
         fill(1, 2)
-        multiply(2, 3)
-        multiply(3, 3)
+        for b, d in ((3, 2), (2, 3), (3, 3)):
+            multiply(b, d)
+        turn_back(0, SHARED_COLS, U)
+
+        fetch(1, 1, 0, U)
+        look_up(2, 0)
+        turn(1, 0, 0, U)
         fill(1, 3)
-        multiply(3, 2)
-        chain(2, 0, 0, 512)
-        turn(0)
-        turn(1)
-        fetch(1, 2, 0, 512)
-        chain(3, 0, 0, 512)
-        turn(2)
-        fetch(1, 3, 0, 512)
-        chain(2, 1, 0, 512)
-        turn(3)
-        fill(2, 2)
-        fill(2, 3)
+        fetch(1, 2, 0, U)
+        look_up(3, 0)
+        turn(1, 1, 0, U)
+        look_up(2, 1)
+        turn(1, 2, 0, U)
+        finish(0, SHARED_COLS, U)
+        fetch(1, 3, 0, HALF_OUT)
         fill(3, 2)
+        fetch(1, 3, HALF_OUT, U)
+        look_up(3, 1)
+        turn(1, 3, 0, HALF_OUT)
+        turn(1, 3, HALF_OUT, U)
+
+        fill(2, 3)
+        turn_back(1, 0, HALF_OUT)
         fill(3, 3)
-        chain(3, 1, 0, 512)
-        turn_back()
-        chain(2, 2, 0, 512)
-        fetch(2, 3, 0, 512)
-        chain(3, 2, 0, 512)
-        fetch(3, 3, 256, 512)
-        chain(2, 3, 0, 512, True)
-        finish()
-        chain(3, 3, 0, 256)
-        chain(3, 3, 256, 512, True)
+        look_up(2, 2)
+        turn_back(1, HALF_OUT, U)
+        fetch(3, 3, HALF_OUT, U)
+        look_up(3, 2)
+        finish(1, 0, HALF_OUT)
+        finish(1, HALF_OUT, U)
+        look_up(2, 3)
+        look_up(3, 3, 0, HALF_OUT)
+        step(3, 3, HALF_OUT, U, found[3, 3, HALF_OUT][:])

@@ -110,7 +110,7 @@ def tile_picked_yadc_dist_p_kernel(
         spread_scales = keep.tile([P, S], U8, name="spread_scales")
         nc.vector.tensor_copy(spread_scales[:], store_scales[:].indirect(picks[:]))
         for r in range(4):
-            nc.sync.dma_start(
+            nc.scalar.dma_start(
                 picked_scales[r:P:32, :].bitcast(I32),
                 spread_scales[32 + 4 * r : 96 : 16, :].bitcast(I32),
             )

@@ -323,6 +323,7 @@ def tile_picked_yadc_dist_p_kernel(
         look_up(3, 2)
         finish(1, 0, HALF_OUT)
         finish(1, HALF_OUT, U)
-        look_up(2, 3)
+        look_up(2, 3, 0, HALF_OUT)
+        look_up(2, 3, HALF_OUT, U)
         look_up(3, 3, 0, HALF_OUT)
         step(3, 3, HALF_OUT, U, found[3, 3, HALF_OUT][:])

@@ -197,7 +197,7 @@ def tile_picked_yadc_dist_p_kernel(
                 nc.vector.tensor_tensor(sums[b, d][:, cols], values, norm_rows[:, cols], SUBTRACT)
             else:
                 nc.vector.tensor_tensor(sums[b, d][:, cols], values, sums[b, d - 1][:, cols], ADD)
-            if d == BOOKS - 1:
+            if d == BOOKS - 1 and b != BATCHES - 1:
                 nc.sync.dma_start(out[b * P : (b + 1) * P, cols], sums[b, d][:, cols])
 
         def look_up(b, d, lo=0, hi=U):
@@ -327,3 +327,4 @@ def tile_picked_yadc_dist_p_kernel(
         look_up(2, 3, HALF_OUT, U)
         look_up(3, 3, 0, HALF_OUT)
         step(3, 3, HALF_OUT, U, found[3, 3, HALF_OUT][:])
+        nc.sync.dma_start(out[3 * P :, :], sums[3, 3][:])

from contextlib import ExitStack

import concourse.mybir as mybir
from concourse.masks import make_identity

K, T, S, V, U, R = 512, 4096, 1024, 512, 512, 256
BOOKS = 4
FLOPS = 2 * K * V * S

F32 = mybir.dt.float32
BF16 = mybir.dt.bfloat16
I32 = mybir.dt.int32
U32 = mybir.dt.uint32
U16 = mybir.dt.uint16
U8 = mybir.dt.uint8
FP8X4 = mybir.dt.float8_e4m3fn_x4
ADD = mybir.AluOpType.add
SUBTRACT = mybir.AluOpType.subtract
COPY = mybir.ActivationFunctionType.Copy

P = 128
PACK = 4
LIST_ROWS = 16
BATCHES = V // P
HALF_PICKS = S // 2
HALF_OUT = U // 2
SCALAR_BATCH = 1
SHARED_COLS = U - P
SHARED_HALF = SHARED_COLS // 2
SPARE = 16
VECTOR_SHARE = 520
ODD_REST = 7

BANK_OF = {
    (0, 0): 0, (0, 1): 1, (0, 2): 2, (1, 0): 3, (0, 3): 4,
    (2, 0): 0, (3, 0): 1, (2, 1): 2, (3, 1): 3, (2, 2): 4,
    (1, 1): 0, (1, 2): 1, (1, 3): 2,
    (3, 2): 6, (2, 3): 7, (3, 3): 0,
}
GROUP_BANK = {(0, SHARED_COLS): 5, (SCALAR_BATCH, 0): 3, (SCALAR_BATCH, HALF_OUT): 4}

FIRST_WORDS_AT = 2048
GROUPED0_AT = 3584
SCALE_TABLE_AT = 4096
NORM_AT = 4608
RAW23_AT = NORM_AT + 4 * U
GROUPED23_AT = 12288
LAST_FETCH_AT = 16384


def tile_picked_yadc_dist_p_kernel(
    tc, x_words, x_scales, hT, norm, offs, code1, code2, code3, code4, out
):
    nc = tc.nc
    with ExitStack() as ctx:
        keep = ctx.enter_context(tc.tile_pool(name="keep", bufs=1))
        late = ctx.enter_context(tc.tile_pool(name="late", bufs=1))
        early = ctx.enter_context(tc.tile_pool(name="early", bufs=1))
        psum = ctx.enter_context(tc.psum_pool(name="psum", bufs=1))

        picks = keep.tile([P, S // LIST_ROWS], U16, name="picks")
        nc.sync.dma_start(picks[:], offs)
        h_rows = hT.rearrange("(p j) t -> p j t", j=PACK)
        raw0 = keep.tile([P, PACK, P], F32, name="raw0")
        nc.sync.dma_start(raw0[:], h_rows[:, :, :P])

        codes = [keep.tile([P, U // LIST_ROWS], U16, name="code%d" % d) for d in range(BOOKS)]
        for tile, code in zip(codes[:2], (code1, code2)):
            nc.sync.dma_start(tile[:], code)

        def table_width(b, d):
            longest = SHARED_COLS if b == 0 else U
            return 2 * longest if b != SCALAR_BATCH and d == 0 else longest + SPARE

        tables = {
            (b, d): keep.tile([P, table_width(b, d)], F32, name="table%d_%d" % (b, d))
            for b in range(BATCHES)
            for d in range(BOOKS)
        }

        zeros = early.tile([P, SPARE - 1], F32, name="zeros", offset=4 * T - 32)
        nc.vector.memset(zeros[:], 0.0)
        store_scales = late.tile([P, T], U8, name="store_scales", offset=SCALE_TABLE_AT)
        cleared = store_scales[:].bitcast(U32)
        nc.vector.memset(cleared[:, : VECTOR_SHARE - ODD_REST], 0)
        nc.vector.memset(cleared[:, VECTOR_SHARE - ODD_REST : VECTOR_SHARE], 0)
        nc.gpsimd.memset(cleared[:, VECTOR_SHARE:], 0)
        nc.sync.dma_start(store_scales[32:96:4, :].bitcast(I32), x_scales[0].bitcast(I32))
        nc.vector.tensor_copy(tables[0, 1][:, SHARED_COLS + 1 :], zeros[:])
        store_words = early.tile([P, T], U32, name="store_words", offset=0)
        word_rows = x_words[0].rearrange("p n t -> p (n t)").bitcast(I32)
        for lo in range(0, T, T // 2):
            nc.sync.dma_start(store_words[:, lo : lo + T // 2].bitcast(I32), word_rows[:, lo : lo + T // 2])
        raw1 = early.tile([P, PACK, P], F32, name="raw1", offset=4 * T)
        nc.sync.dma_start(raw1[:], h_rows[:, :, P : 2 * P])

        for tile, code in zip(codes[2:], (code3, code4)):
            nc.sync.dma_start(tile[:], code)

        picked_scales = keep.tile([P, S], U8, name="picked_scales", align_bytes=64)
        nc.vector.memset(picked_scales[:].bitcast(I32), 0)
        nc.vector.memset(tables[3, 0][:, R:], 0.0)
        for key, table in tables.items():
            if key != (3, 0):
                end = SHARED_COLS + 1 if key == (0, 1) else table_width(*key)
                nc.scalar.copy(table[:, R:end], tables[3, 0][:, R:end])
        identity = keep.tile([P, P], F32, name="identity")
        make_identity(nc, identity[:])

        spread_scales = keep.tile([P, S], U8, name="spread_scales")
        nc.vector.tensor_copy(spread_scales[:], store_scales[:].indirect(picks[:]))
        for r in range(4):
            nc.scalar.dma_start(
                picked_scales[r:P:32, :].bitcast(I32),
                spread_scales[32 + 4 * r : 96 : 16, :].bitcast(I32),
            )

        norm_rows = late.tile([P, U], F32, name="norm_rows", offset=NORM_AT)
        nc.sync.dma_start(norm_rows[:], norm)
        raw23 = late.tile([P, PACK, 2 * P], F32, name="raw23", offset=RAW23_AT)
        nc.sync.dma_start(raw23[:], h_rows[:, :, 2 * P :])
        raws = [raw0, raw1, raw23]

        h_codes = keep.tile([P, V], U32, name="h_codes", align_bytes=64)
        h_scales = keep.tile([P, V], U8, name="h_scales", align_bytes=64)

        grouped, banks, sums, found, groups, backs = {}, {}, {}, {}, {}, {}

        def pick_words(h):
            cols = HALF_PICKS // LIST_ROWS
            nc.vector.tensor_copy(picked_words[h][:], store_words[:].indirect(picks[:, h * cols : (h + 1) * cols]))

        def interleave(b, copy):
            if b == 0:
                grouped[b] = late.tile([P, P, PACK], BF16, name="grouped0", offset=GROUPED0_AT, align_bytes=64)
            elif b == 1:
                grouped[b] = keep.tile([P, P, PACK], BF16, name="grouped1", align_bytes=64)
            else:
                grouped[b] = late.tile([P, 2 * P, PACK], BF16, name="grouped23", offset=GROUPED23_AT, align_bytes=64)
            copy(
                grouped[b][:].rearrange("p (c i) j -> p c j i", i=4),
                raws[b][:].rearrange("p j (c i) -> p c j i", i=4),
            )

        def quantise(b):
            cols = slice(b * P, b * P + grouped[b].shape[1])
            nc.vector.quantize_mx(
                out=h_codes[:, cols].bitcast(FP8X4),
                scales=h_scales[:, cols],
                in_=grouped[b][:].rearrange("p t j -> p (t j)"),
            )

        def multiply(b, d):
            banks[b, d] = psum.tile([P, R], F32, name="bank", tag="bank%d" % BANK_OF[b, d])
            nc.tensor.matmul_mx(
                out=banks[b, d][:],
                lhsT=h_codes[:, b * P : (b + 1) * P].bitcast(FP8X4),
                lhsT_scale=h_scales[:, b * P : (b + 1) * P],
                rhs=picked_words[d // 2][:, d % 2 * R : (d % 2 + 1) * R].bitcast(FP8X4),
                rhs_scale=picked_scales[:, d * R : (d + 1) * R],
                start=True,
                stop=True,
            )

        def fill(b, d):
            if b == SCALAR_BATCH:
                nc.scalar.mul(tables[b, d][:, :R], banks[b, d][:], -1.0)
            else:
                nc.scalar.copy(tables[b, d][:, :R], banks[b, d][:])

        def entries(b, d, lo, hi):
            return tables[b, d][:].indirect(codes[d][:, lo // LIST_ROWS : hi // LIST_ROWS])

        def fetch(b, d, lo, hi):
            name = "found%d_%d_%d" % (b, d, lo)
            if d == BOOKS - 1 and lo == HALF_OUT:
                found[b, d, lo] = late.tile([P, hi - lo], F32, name=name, offset=LAST_FETCH_AT)
            else:
                found[b, d, lo] = keep.tile([P, hi - lo], F32, name=name)
            if b == 0:
                nc.scalar.activation(found[b, d, lo][:], entries(b, d, lo, hi), COPY, scale=-1.0)
            else:
                nc.scalar.activation(found[b, d, lo][:], entries(b, d, lo, hi), COPY)

        def sum_tile(b, d):
            if (b, d) == (0, 1):
                return late.tile([P, SHARED_COLS], F32, name="sum0_1", offset=RAW23_AT)
            if (b, d) == (0, 2):
                return late.tile([P, SHARED_COLS], F32, name="sum0_2", offset=GROUPED23_AT)
            return keep.tile([P, U], F32, name="sum%d_%d" % (b, d))

        def step(b, d, lo, hi, values):
            cols = slice(lo, hi)
            if (b, d) not in sums:
                sums[b, d] = sum_tile(b, d)
            if d == 0:
                nc.vector.tensor_tensor(sums[b, d][:, cols], values, norm_rows[:, cols], SUBTRACT)
            else:
                nc.vector.tensor_tensor(sums[b, d][:, cols], values, sums[b, d - 1][:, cols], ADD)
            if d == BOOKS - 1 and b != BATCHES - 1:
                nc.sync.dma_start(out[b * P : (b + 1) * P, cols], sums[b, d][:, cols])

        def look_up(b, d, lo=0, hi=U):
            step(b, d, lo, hi, entries(b, d, lo, hi))

        def look_up_in_halves(d):
            for lo in (0, SHARED_HALF):
                look_up(0, d, lo, lo + SHARED_HALF)

        def add_to_group(b, at, width, source, first, last):
            if first:
                groups[b, at] = psum.tile([P, width], F32, name="group", tag="bank%d" % GROUP_BANK[b, at])
            for c in range(0, width, P):
                nc.tensor.matmul(
                    groups[b, at][:, c : c + P],
                    source[:, c : c + P],
                    identity[:],
                    is_transpose=True,
                    start=(first and c == 0),
                    stop=(last and c == width - P),
                )

        def turn(b, d, lo, hi):
            width = min(hi - lo, HALF_OUT)
            for at in range(lo, hi, width):
                norm_first = d == 0 and b == SCALAR_BATCH
                if norm_first:
                    add_to_group(b, at, width, norm_rows[:, at : at + width], True, False)
                source = found[b, d, lo][:, at - lo : at - lo + width]
                add_to_group(b, at, width, source, d == 0 and not norm_first, d == BOOKS - 1)
                if d == 1 and b == 0:
                    add_to_group(b, at, width, norm_rows[:, at : at + width], False, False)

        def turn_back(b, lo, hi):
            name = "middle%d_%d" % (b, lo)
            if b == 0:
                middle = late.tile([P, hi - lo], F32, name=name, offset=FIRST_WORDS_AT)
            else:
                middle = keep.tile([P, hi - lo], F32, name=name)
            nc.scalar.copy(middle[:], groups[b, lo][:])
            backs[b, lo] = psum.tile([P, hi - lo], F32, name="back", tag="bank%d" % GROUP_BANK[b, lo])
            for c in range(0, hi - lo, P):
                nc.tensor.transpose(backs[b, lo][:, c : c + P], middle[:, c : c + P], identity[:])

        def finish(b, lo, hi):
            result = keep.tile([P, hi - lo], F32, name="result%d_%d" % (b, lo))
            nc.scalar.mul(result[:], backs[b, lo][:], -1.0)
            queue = nc.sync if b == 0 else nc.scalar
            queue.dma_start(out[b * P : (b + 1) * P, lo:hi], result[:])

        interleave(0, nc.vector.tensor_copy)
        quantise(0)
        picked_words = [
            late.tile([P, HALF_PICKS], U32, name="picked_words0", offset=FIRST_WORDS_AT, align_bytes=64),
            keep.tile([P, HALF_PICKS], U32, name="picked_words1", align_bytes=64),
        ]
        pick_words(0)
        pick_words(1)
        interleave(1, nc.scalar.copy)
        quantise(1)

        for d in range(BOOKS):
            multiply(0, d)
        multiply(1, 0)
        fill(0, 0)
        fill(0, 1)
        fetch(0, 0, SHARED_COLS, U)
        look_up(0, 0, 0, SHARED_COLS)
        fill(0, 2)
        fill(0, 3)
        interleave(2, nc.vector.tensor_copy)
        fetch(0, 1, SHARED_COLS, U)
        fetch(0, 2, SHARED_COLS, U)
        fill(1, 0)
        turn(0, 0, SHARED_COLS, U)
        turn(0, 1, SHARED_COLS, U)
        look_up(0, 1, 0, SHARED_HALF)
        fetch(0, 3, SHARED_COLS, U)
        quantise(2)
        look_up(0, 1, SHARED_HALF, SHARED_COLS)
        fetch(1, 0, 0, U)
        turn(0, 2, SHARED_COLS, U)
        turn(0, 3, SHARED_COLS, U)

        run = [(2, 0), (3, 0), (2, 1), (3, 1), (2, 2)]
        for b, d in run:
            multiply(b, d)
        look_up_in_halves(2)
        for i, (b, d) in enumerate(run):
            fill(b, d)
            if i + 1 < BOOKS:
                multiply(1, i + 1)
        look_up_in_halves(3)
        fill(1, 1)
        fill(1, 2)
        for b, d in ((3, 2), (2, 3), (3, 3)):
            multiply(b, d)
        turn_back(0, SHARED_COLS, U)

        fetch(1, 1, 0, U)
        look_up(2, 0)
        turn(1, 0, 0, U)
        fill(1, 3)
        fetch(1, 2, 0, U)
        look_up(3, 0)
        turn(1, 1, 0, U)
        look_up(2, 1)
        turn(1, 2, 0, U)
        finish(0, SHARED_COLS, U)
        fetch(1, 3, 0, HALF_OUT)
        fill(3, 2)
        fetch(1, 3, HALF_OUT, U)
        look_up(3, 1)
        turn(1, 3, 0, HALF_OUT)
        turn(1, 3, HALF_OUT, U)

        fill(2, 3)
        turn_back(1, 0, HALF_OUT)
        fill(3, 3)
        look_up(2, 2)
        turn_back(1, HALF_OUT, U)
        fetch(3, 3, HALF_OUT, U)
        look_up(3, 2)
        finish(1, 0, HALF_OUT)
        finish(1, HALF_OUT, U)
        look_up(2, 3, 0, HALF_OUT)
        look_up(2, 3, HALF_OUT, U)
        look_up(3, 3, 0, HALF_OUT)
        step(3, 3, HALF_OUT, U, found[3, 3, HALF_OUT][:])
        nc.sync.dma_start(out[3 * P :, :], sums[3, 3][:])
